import numpy as np
import ml_dtypes


def mxq(x, axis, fmt="e4m3"):
    dtype, down = {"e4m3": (ml_dtypes.float8_e4m3fn, 7), "e5m2": (ml_dtypes.float8_e5m2, 14)}[fmt]
    v = np.moveaxis(np.asarray(x, np.float32).astype(ml_dtypes.bfloat16).astype(np.float64), axis, -1)
    blocks = v.reshape(v.shape[:-1] + (-1, 32))
    amax = np.abs(blocks).max(-1, keepdims=True)
    byte = np.maximum(np.where(amax > 0, np.frexp(amax)[1] - 1 + 127, 0) - down, 1)
    scale = np.exp2(byte - 127.0)
    codes = (blocks / scale).astype(np.float32).astype(dtype).astype(np.float64)
    return np.moveaxis((codes * scale).reshape(v.shape), -1, axis)


WIDE = False


def mx_kscale(k):
    if not WIDE:
        return np.ones(k)
    levels = np.array([10, -10, 5, -5, 0])
    if k % 512:
        return np.exp2(np.random.permutation(np.resize(levels, k // 32))).repeat(32)
    a = np.empty((k // 512, 16))
    for p in range(k // 512):
        a[p, :8] = np.random.permutation(np.resize(levels, 8))
        for g in range(8):
            far = levels[np.abs(levels - a[p, g]) >= 10]
            a[p, g + 8] = far[np.random.randint(len(far))]
    return np.exp2(a.ravel()).repeat(32)


BF16 = ml_dtypes.bfloat16


def bf(x):
    return np.asarray(x, np.float32).astype(BF16)


def f64(x):
    return np.asarray(x).astype(np.float64)


E2M1 = np.array([0.0, 0.5, 1.0, 1.5, 2.0, 3.0, 4.0, 6.0, -0.0, -0.5, -1.0, -1.5, -2.0, -3.0, -4.0, -6.0])


def pack_weight(w, fmt):
    k, n = w.shape
    w = f64(bf(w)).reshape(k // 32, 32, n)
    amax = np.abs(w).max(1)
    if fmt == "e4m3":
        byte = np.frexp(amax)[1] - 1 + 127 - 7
    else:
        mant, ex = np.frexp(amax / 6.0)
        byte = np.where(mant > 0.5, ex, ex - 1) + 127
    byte = np.clip(np.where(amax > 0, byte, 1), 1, 254)
    scaled = (w * np.exp2(127.0 - byte)[:, None, :]).reshape(k, n).astype(np.float32)
    by_word = np.ascontiguousarray(scaled.reshape(k // 512, 128, 4, n).transpose(0, 1, 3, 2))
    if fmt == "e4m3":
        words = by_word.astype(ml_dtypes.float8_e4m3fn).view(np.uint8)
    else:
        c = by_word.astype(ml_dtypes.float4_e2m1fn).view(np.uint8) & 0xF
        words = c[..., 0::2] | (c[..., 1::2] << 4)
    return np.ascontiguousarray(words), np.ascontiguousarray(byte.astype(np.uint8).reshape(k // 512, 16, n))


def unpack_weight(words, scales, fmt):
    g, p, n, _ = words.shape
    if fmt == "e4m3":
        vals = np.ascontiguousarray(words).view(ml_dtypes.float8_e4m3fn).astype(np.float64)
    else:
        nib = np.empty((g, p, n, 4), np.uint8)
        nib[..., 0::2] = words & 0xF
        nib[..., 1::2] = words >> 4
        vals = E2M1[nib]
    vals = vals * np.repeat(np.exp2(scales.astype(np.float64) - 127.0), 8, axis=1)[..., None]
    return vals.transpose(0, 1, 3, 2).reshape(g * 512, n)
def pack4(w):
    words, scales = pack_weight(w, "e2m1")
    return words.reshape(words.shape[0], 128, -1), scales


def unpack4(words, scales):
    return unpack_weight(words.reshape(words.shape[0], 128, -1, 2), scales, "e2m1")


def planes(Y):
    n, m = Y.shape
    b = f64(bf(Y)).reshape(n // 32, 32, m)
    amax = np.abs(b).max(1)
    byte = np.clip(np.where(amax > 0, np.frexp(amax)[1] - 1 + 127 - 7, 1), 1, 254)
    codes = (b * np.exp2(127.0 - byte)[:, None, :]).reshape(n, m).astype(np.float32).astype(ml_dtypes.float8_e4m3fn).view(np.uint8)
    words = codes.reshape(n // 512, 128, 4, m).transpose(0, 1, 3, 2)
    return np.ascontiguousarray(words), np.ascontiguousarray(byte.astype(np.uint8).reshape(n // 512, 16, m))


Z, R, E, F = 4, 768, 512, 1024

def setup_inputs():
    s = mx_kscale(Z * E)
    t = mx_kscale(Z * F)
    room = np.random.randn(Z, F, E) / np.sqrt(F)
    inverse = np.linalg.pinv(room)
    x = bf(np.random.randn(Z, R, E) * s.reshape(Z, 1, E))
    c_words, c_scales = pack4(inverse.reshape(Z * E, F) / s[:, None])
    ceiling = bf((1 + 0.1 * np.random.randn(Z, F)) * t.reshape(Z, F))
    h_words, h_scales = pack4(room.reshape(Z * F, E) / t[:, None])
    bypass = bf(0.5 * np.random.randn(Z, R, E))
    ear_gain = bf(np.exp(0.8 * np.random.randn(Z, E)))
    return dict(x=x, c_words=c_words, c_scales=c_scales, ceiling=ceiling,
                h_words=h_words, h_scales=h_scales, bypass=bypass, ear_gain=ear_gain)

def reference(x, c_words, c_scales, ceiling, h_words, h_scales, bypass, ear_gain):
    C = unpack4(c_words, c_scales).reshape(Z, E, F)
    H = unpack4(h_words, h_scales).reshape(Z, F, E)
    u = mxq(f64(x), 2, "e4m3") @ C
    d = np.tanh(u) * f64(ceiling)[:, None, :]
    v = mxq(d, 2, "e4m3") @ H
    y = (v + f64(bypass)) * f64(ear_gain)[:, None, :]
    Y = y.transpose(2, 0, 1).reshape(E, Z * R)
    words, scales = planes(Y)
    return y, words, scales

@@ -1,0 +1,346 @@
+from contextlib import ExitStack
+
+import concourse.mybir as mybir
+from concourse.masks import make_identity
+
+Z, R, E, F = 4, 768, 512, 1024
+FLOPS = 2 * 2 * Z * R * E * F
+
+F32 = mybir.dt.float32
+BF16 = mybir.dt.bfloat16
+I32 = mybir.dt.int32
+U32 = mybir.dt.uint32
+U8 = mybir.dt.uint8
+FP8X4 = mybir.dt.float8_e4m3fn_x4
+FP4X4 = mybir.dt.float4_e2m1fn_x4
+ACT = mybir.ActivationFunctionType
+ALU = mybir.AluOpType
+
+P = 128
+GROUP = 256
+TILES = GROUP // P
+GROUPS = Z * R // GROUP
+GROUPS_PER_SEAT = R // GROUP
+PASSES = F // 512
+DRIVE_BANKS = 3
+SHIFT_ROWS = 112
+
+
+def tile_seatwise_crosstalk_canceller_k7_kernel(
+    tc, x, c_words, c_scales, ceiling, h_words, h_scales, bypass, ear_gain, out_0, out_1, out_2
+):
+    nc = tc.nc
+    x_rows = x.rearrange("z r e -> (z r) e")
+    bypass_rows = bypass.rearrange("z r e -> (z r) e")
+    y_rows = out_0.rearrange("z r e -> (z r) e")
+    y_words = out_1[0].rearrange("p m t -> p (m t)").bitcast(I32)
+    y_scale_rows = out_2[0]
+
+    with ExitStack() as ctx:
+        sb = ctx.enter_context(tc.tile_pool(name="sb", bufs=1))
+        ps = ctx.enter_context(tc.psum_pool(name="ps", bufs=1))
+        ctx.enter_context(tc.manual_schedule())
+
+        def ring(name, count, shape, dtype):
+            return [sb.tile(shape, dtype, name="%s%d" % (name, i), align_bytes=64) for i in range(count)]
+
+        ident = sb.tile([P, P], F32, name="ident", align_bytes=64)
+        warm = sb.tile([P, 1], F32, name="warm", align_bytes=64)
+        x_sb = ring("x", GROUPS, [P, TILES, E], BF16)
+        bypass_sb = ring("bypass", GROUPS, [P, TILES, E], BF16)
+        y_sb = ring("y", GROUPS, [P, TILES, E], F32)
+        c_raw = ring("c_raw", Z, [P, 2 * F], U8)
+        c_sb = ring("c", Z, [P, 2 * F], U8)
+        cs_raw = sb.tile([P, F], U8, name="cs_raw", align_bytes=64)
+        cs_sb = ring("cs", Z, [P, F], U8)
+        h_sb = ring("h", Z, [P, PASSES, 2 * E], U8)
+        hs_sb = sb.tile([P, Z * PASSES, E], U8, name="hs", align_bytes=64)
+        gain_sb = ring("gain", Z, [P, E], BF16)
+        ceil_rows = sb.tile([P, 512], BF16, name="ceil_rows", align_bytes=64)
+        ceil_f32 = sb.tile([P, 512], F32, name="ceil_f32", align_bytes=64)
+        xg = ring("xg", 2, [P, GROUP * 4], BF16)
+        x_codes = ring("x_codes", 3, [P, GROUP], U32)
+        x_scales = ring("x_scales", 3, [P, GROUP], U8)
+        th = ring("th", 4, [P, 2, GROUP, 2], F32)
+        d_bf = ring("d_bf", 2, [P, PASSES, GROUP * 4], BF16)
+        d_codes = ring("d_codes", 2, [P, PASSES, GROUP], U32)
+        d_scales = ring("d_scales", 2, [P, PASSES, GROUP], U8)
+        s_sb = ring("s", 3, [P, E], F32)
+        y_bf = ring("y_bf", 2, [P, TILES, E], BF16)
+        yg = ring("yg", 2, [P, GROUP * 4], BF16)
+        y_codes = sb.tile([P, Z * R], U32, name="y_codes", align_bytes=64)
+        y_scales = sb.tile([P, Z * R], U8, name="y_scales", align_bytes=64)
+
+        ceil_ps = ps.tile([P, 512], F32, name="ceil_ps")
+        x_ps = ps.tile([P, 512], F32, name="x_ps")
+        y_ps = ps.tile([P, 512], F32, name="y_ps")
+        u_ps = [ps.tile([P, 512], F32, name="u_ps%d" % i) for i in range(DRIVE_BANKS)]
+        v_ps = [ps.tile([P, 512], F32, name="v_ps%d" % i) for i in range(TILES)]
+
+        def seat(i):
+            return i // GROUPS_PER_SEAT
+
+        def group_rows(rows, i):
+            return rows[i * GROUP : (i + 1) * GROUP, :].rearrange("(j p) e -> p j e", p=P)
+
+        def load_x(i):
+            nc.sync.dma_start(out=x_sb[i][:], in_=group_rows(x_rows, i))
+
+        def load_bypass(i):
+            nc.sync.dma_start(out=bypass_sb[i][:], in_=group_rows(bypass_rows, i))
+
+        def load_c(z):
+            nc.sync.dma_start(out=c_raw[z][:].bitcast(I32), in_=c_words[z].bitcast(I32))
+
+        def load_h(z):
+            nc.sync.dma_start(
+                out=h_sb[z][:].bitcast(I32),
+                in_=h_words[PASSES * z : PASSES * (z + 1)].rearrange("g p n -> p g n").bitcast(I32),
+            )
+
+        def load_gain(z):
+            nc.sync.dma_start(out=gain_sb[z][:], in_=ear_gain[z].partition_broadcast(P))
+
+        def shift_c_scales(z):
+            nc.sync.dma_start(
+                out=cs_sb[z][0:SHIFT_ROWS, :].bitcast(I32),
+                in_=cs_sb[0][4 * z : 4 * z + SHIFT_ROWS, :].bitcast(I32),
+            )
+
+        def permute_c(z, g):
+            cols = slice(g * 1024, (g + 1) * 1024)
+            nc.vector.tensor_copy(
+                out=c_sb[z][:, cols].rearrange("p (t m b) -> p t m b", t=4, b=2),
+                in_=c_raw[z][:, cols].rearrange("p (m t b) -> p t m b", t=4, b=2),
+            )
+
+        def permute_c_scales(g):
+            cols = slice(g * 512, (g + 1) * 512)
+            nc.vector.tensor_copy(
+                out=cs_sb[0][:, cols].rearrange("p (t m) -> p t m", t=4),
+                in_=cs_raw[:, cols].rearrange("p (m t) -> p t m", t=4),
+            )
+
+        def turn_x(i):
+            for j in range(TILES):
+                words = x_sb[i][:, j, :].bitcast(F32)
+                for u in range(2):
+                    col = (2 * j + u) * P
+                    nc.tensor.transpose(x_ps[:, col : col + P], words[:, u : 2 * P : 2], ident[:])
+
+        def gather_words(dst, bank):
+            nc.scalar.copy(
+                out=dst[:].bitcast(F32).rearrange("p (j r u) -> p j r u", j=TILES, u=2),
+                in_=bank[:].rearrange("p (j u r) -> p j r u", j=TILES, u=2),
+            )
+
+        def quantize_x(i):
+            nc.vector.quantize_mx(out=x_codes[i % 3][:].bitcast(FP8X4), scales=x_scales[i % 3][:], in_=xg[i % 2][:])
+
+        def drive(i, b):
+            z, g, u = seat(i), b // 2, b % 2
+            bank = u_ps[(4 * i + b) % DRIVE_BANKS]
+            for e in range(2):
+                col = g * 512 + (2 * u + e) * P
+                nc.tensor.matmul_mx(
+                    out=bank[:, e * GROUP : (e + 1) * GROUP],
+                    lhsT=c_sb[z][:, 2 * col : 2 * (col + P)].bitcast(FP4X4),
+                    lhsT_scale=cs_sb[z][:, col : col + P],
+                    rhs=x_codes[i % 3][:].bitcast(FP8X4),
+                    rhs_scale=x_scales[i % 3][:],
+                    start=True,
+                    stop=True,
+                )
+
+        def limit(i, b):
+            bank = u_ps[(4 * i + b) % DRIVE_BANKS]
+            nc.scalar.activation(
+                out=th[(2 * i + b // 2) % 4][:, b % 2, :, :],
+                in_=bank[:].rearrange("p (e n) -> p n e", e=2),
+                func=ACT.Tanh,
+            )
+
+        def apply_ceiling(i, g):
+            row = PASSES * seat(i) + g
+            ceil = ceil_ps[:].rearrange("p (u e r) -> p r u e", u=2, e=2)[:, row : row + 1, :, :]
+            nc.vector.tensor_tensor(
+                out=d_bf[i % 2][:, g, :].rearrange("p (n u e) -> p n u e", u=2, e=2),
+                in0=th[(2 * i + g) % 4][:].rearrange("p u n e -> p n u e"),
+                in1=ceil.to_broadcast([P, GROUP, 2, 2]),
+                op=ALU.mult,
+            )
+
+        def quantize_d(i):
+            nc.vector.quantize_mx(
+                out=d_codes[i % 2][:].rearrange("p g n -> p (g n)").bitcast(FP8X4),
+                scales=d_scales[i % 2][:].rearrange("p g n -> p (g n)"),
+                in_=d_bf[i % 2][:].rearrange("p g n -> p (g n)"),
+            )
+
+        def room(i, j):
+            z = seat(i)
+            for g in range(PASSES):
+                nc.tensor.matmul_mx(
+                    out=v_ps[j][:],
+                    lhsT=d_codes[i % 2][:, g, j * P : (j + 1) * P].bitcast(FP8X4),
+                    lhsT_scale=d_scales[i % 2][:, g, j * P : (j + 1) * P],
+                    rhs=h_sb[z][:, g, :].bitcast(FP4X4),
+                    rhs_scale=hs_sb[:, PASSES * z + g, :],
+                    start=(g == 0),
+                    stop=(g == PASSES - 1),
+                )
+
+        def add_bypass(i, j):
+            nc.vector.tensor_tensor(
+                out=s_sb[(2 * i + j) % 3][:], in0=v_ps[j][:], in1=bypass_sb[i][:, j, :], op=ALU.add
+            )
+
+        def apply_gain(i, j):
+            nc.gpsimd.tensor_tensor(
+                out=y_sb[i][:, j, :], in0=s_sb[(2 * i + j) % 3][:], in1=gain_sb[seat(i)][:], op=ALU.mult
+            )
+
+        def round_y(i, j):
+            nc.scalar.copy(
+                out=y_bf[i % 2][:, j, :].rearrange("p (u m e) -> p u m e", u=2, e=2),
+                in_=y_sb[i][:, j, :].rearrange("p (m u e) -> p u m e", u=2, e=2),
+            )
+
+        def turn_y(i):
+            for j in range(TILES):
+                words = y_bf[i % 2][:, j, :].bitcast(F32)
+                for u in range(2):
+                    col = (2 * j + u) * P
+                    nc.tensor.transpose(y_ps[:, col : col + P], words[:, u * P : (u + 1) * P], ident[:])
+
+        def quantize_y(i):
+            cols = slice(i * GROUP, (i + 1) * GROUP)
+            nc.vector.quantize_mx(out=y_codes[:, cols].bitcast(FP8X4), scales=y_scales[:, cols], in_=yg[i % 2][:])
+
+        def store_y(i):
+            nc.sync.dma_start(out=group_rows(y_rows, i), in_=y_sb[i][:])
+
+        def store_codes(i):
+            cols = slice(i * GROUP, (i + 1) * GROUP)
+            nc.sync.dma_start(out=y_words[:, cols], in_=y_codes[:, cols].bitcast(I32))
+
+        def store_scales(first, last):
+            cols = slice(first * GROUP, (last + 1) * GROUP)
+            for q in range(4):
+                nc.sync.dma_start(
+                    out=y_scale_rows[4 * q : 4 * q + 4, cols].bitcast(I32),
+                    in_=y_scales[32 * q : 32 * q + 4, cols].bitcast(I32),
+                )
+
+        nc.vector.memset(cs_raw[:].bitcast(I32), 0)
+        nc.vector.memset(warm[:], 0.0)
+        nc.vector.memset(ceil_f32[:], 0.0)
+        make_identity(nc, ident[:])
+        nc.gpsimd.memset(hs_sb[:].rearrange("p g n -> p (g n)").bitcast(I32), 0)
+        for z in range(1, Z):
+            nc.gpsimd.memset(cs_sb[z][:].bitcast(I32), 0)
+
+        load_x(0)
+        load_c(0)
+        for q in range(4):
+            nc.scalar.dma_start(
+                out=cs_raw[32 * q : 32 * q + 16, :].bitcast(I32),
+                in_=c_scales[:, 4 * q : 4 * q + 4, :].bitcast(I32),
+            )
+        nc.scalar.activation(out=warm[:], in_=warm[:], func=ACT.Tanh)
+        nc.sync.dma_start(
+            out=ceil_rows[0 : Z * PASSES, :], in_=ceiling.rearrange("z (g f) -> (z g) f", g=PASSES)
+        )
+        load_x(1)
+        load_x(2)
+        load_c(1)
+        for q in range(4):
+            nc.sync.dma_start(
+                out=hs_sb[32 * q : 32 * q + 4, :, :].bitcast(I32),
+                in_=h_scales[:, 4 * q : 4 * q + 4, :].rearrange("g r n -> r g n").bitcast(I32),
+            )
+        load_h(0)
+        load_x(3)
+        load_bypass(0)
+        load_gain(0)
+
+        permute_c_scales(0)
+        permute_c(0, 0)
+        nc.vector.tensor_copy(out=ceil_f32[0 : Z * PASSES, :], in_=ceil_rows[0 : Z * PASSES, :])
+
+        def live(i):
+            return 0 <= i < GROUPS
+
+        for k in range(-3, GROUPS + 3):
+            if live(k - 2):
+                add_bypass(k - 2, 0)
+            if live(k - 3):
+                gather_words(yg[(k - 3) % 2], y_ps)
+            if live(k + 1):
+                for b in range(3):
+                    drive(k + 1, b)
+            if live(k - 2):
+                add_bypass(k - 2, 1)
+                apply_gain(k - 2, 0)
+            if live(k + 2):
+                gather_words(xg[(k + 2) % 2], x_ps)
+            if live(k - 1):
+                room(k - 1, 0)
+            if live(k):
+                apply_ceiling(k, 0)
+            if live(k - 2):
+                apply_gain(k - 2, 1)
+                store_y(k - 2)
+            if live(k + 1):
+                limit(k + 1, 0)
+                limit(k + 1, 1)
+            if live(k + 3):
+                turn_x(k + 3)
+            if k == -2:
+                for t in range(4):
+                    nc.tensor.transpose(ceil_ps[:, t * P : (t + 1) * P], ceil_f32[:, t : 512 : 4], ident[:])
+            if live(k):
+                apply_ceiling(k, 1)
+            if live(k - 2):
+                round_y(k - 2, 0)
+            if live(k + 1):
+                drive(k + 1, 3)
+            if live(k - 1):
+                room(k - 1, 1)
+            if live(k + 1):
+                limit(k + 1, 2)
+            if live(k - 3):
+                quantize_y(k - 3)
+                store_codes(k - 3)
+            if live(k + 2):
+                quantize_x(k + 2)
+            if k == -2:
+                permute_c_scales(1)
+                permute_c(0, 1)
+            if k == -1:
+                permute_c(1, 0)
+                permute_c(1, 1)
+                for z in range(1, Z):
+                    shift_c_scales(z)
+            if k in (1, 2, 4, 5):
+                permute_c(2 + k // 4, (k - 1) % 3)
+            if live(k):
+                quantize_d(k)
+            if live(k - 2):
+                round_y(k - 2, 1)
+            if live(k + 1):
+                limit(k + 1, 3)
+            if live(k - 2):
+                turn_y(k - 2)
+            if live(k + 5) and k + 5 > 3:
+                load_x(k + 5)
+            if live(k + 2) and k + 2 > 0:
+                load_bypass(k + 2)
+            if k in (-1, 2):
+                load_c(2 + k // 2 if k > 0 else 2)
+            if k in (0, 3, 6):
+                load_h(k // 3 + 1)
+                load_gain(k // 3 + 1)
+            if k - 3 == GROUPS - 3:
+                store_scales(0, GROUPS - 3)
+        store_scales(GROUPS - 2, GROUPS - 1)

@@ -24,6 +24,10 @@ GROUPS_PER_SEAT = R // GROUP
 PASSES = F // 512
 DRIVE_BANKS = 3
 SHIFT_ROWS = 112
+LAST = GROUPS - 1
+BOTH = slice(0, TILES)
+TILE0 = slice(0, 1)
+TILE1 = slice(1, 2)
 
 
 def tile_seatwise_crosstalk_canceller_k7_kernel(
@@ -49,7 +53,7 @@ def tile_seatwise_crosstalk_canceller_k7_kernel(
         x_sb = ring("x", GROUPS, [P, TILES, E], BF16)
         bypass_sb = ring("bypass", GROUPS, [P, TILES, E], BF16)
         y_sb = ring("y", GROUPS, [P, TILES, E], F32)
-        c_raw = ring("c_raw", Z, [P, 2 * F], U8)
+        c_raw = sb.tile([P, Z, 2 * F], U8, name="c_raw", align_bytes=64)
         c_sb = ring("c", Z, [P, 2 * F], U8)
         cs_raw = sb.tile([P, F], U8, name="cs_raw", align_bytes=64)
         cs_sb = ring("cs", Z, [P, F], U8)
@@ -65,9 +69,9 @@ def tile_seatwise_crosstalk_canceller_k7_kernel(
         d_bf = ring("d_bf", 2, [P, PASSES, GROUP * 4], BF16)
         d_codes = ring("d_codes", 2, [P, PASSES, GROUP], U32)
         d_scales = ring("d_scales", 2, [P, PASSES, GROUP], U8)
-        s_sb = ring("s", 3, [P, E], F32)
+        s_sb = ring("s", 4, [P, E], F32)
         y_bf = ring("y_bf", 2, [P, TILES, E], BF16)
-        yg = ring("yg", 2, [P, GROUP * 4], BF16)
+        yg = ring("yg", 4, [P, GROUP * 4], BF16)
         y_codes = sb.tile([P, Z * R], U32, name="y_codes", align_bytes=64)
         y_scales = sb.tile([P, Z * R], U8, name="y_scales", align_bytes=64)
 
@@ -76,6 +80,12 @@ def tile_seatwise_crosstalk_canceller_k7_kernel(
         y_ps = ps.tile([P, 512], F32, name="y_ps")
         u_ps = [ps.tile([P, 512], F32, name="u_ps%d" % i) for i in range(DRIVE_BANKS)]
         v_ps = [ps.tile([P, 512], F32, name="v_ps%d" % i) for i in range(TILES)]
+
+        def x_stage(i):
+            return y_sb[i - 3][:, 1, :].bitcast(BF16) if i in (3, 4) else xg[i % 2][:]
+
+        def y_stage(i):
+            return y_sb[i + 2][:, 1, :].bitcast(BF16) if i < LAST - 3 else yg[i % 4][:]
 
         def seat(i):
             return i // GROUPS_PER_SEAT
@@ -89,8 +99,10 @@ def tile_seatwise_crosstalk_canceller_k7_kernel(
         def load_bypass(i):
             nc.sync.dma_start(out=bypass_sb[i][:], in_=group_rows(bypass_rows, i))
 
-        def load_c(z):
-            nc.sync.dma_start(out=c_raw[z][:].bitcast(I32), in_=c_words[z].bitcast(I32))
+        def load_c(seats):
+            nc.sync.dma_start(
+                out=c_raw[:, seats, :].bitcast(I32), in_=c_words[seats].rearrange("z p n -> p z n").bitcast(I32)
+            )
 
         def load_h(z):
             nc.sync.dma_start(
@@ -111,7 +123,7 @@ def tile_seatwise_crosstalk_canceller_k7_kernel(
             cols = slice(g * 1024, (g + 1) * 1024)
             nc.vector.tensor_copy(
                 out=c_sb[z][:, cols].rearrange("p (t m b) -> p t m b", t=4, b=2),
-                in_=c_raw[z][:, cols].rearrange("p (m t b) -> p t m b", t=4, b=2),
+                in_=c_raw[:, z, cols].rearrange("p (m t b) -> p t m b", t=4, b=2),
             )
 
         def permute_c_scales(g):
@@ -121,21 +133,21 @@ def tile_seatwise_crosstalk_canceller_k7_kernel(
                 in_=cs_raw[:, cols].rearrange("p (m t) -> p t m", t=4),
             )
 
-        def turn_x(i):
+        def turn_x(i, bank):
             for j in range(TILES):
                 words = x_sb[i][:, j, :].bitcast(F32)
                 for u in range(2):
                     col = (2 * j + u) * P
-                    nc.tensor.transpose(x_ps[:, col : col + P], words[:, u : 2 * P : 2], ident[:])
+                    nc.tensor.transpose(bank[:, col : col + P], words[:, u : 2 * P : 2], ident[:])
 
-        def gather_words(dst, bank):
+        def gather_words(dst, bank, tiles):
             nc.scalar.copy(
-                out=dst[:].bitcast(F32).rearrange("p (j r u) -> p j r u", j=TILES, u=2),
-                in_=bank[:].rearrange("p (j u r) -> p j r u", j=TILES, u=2),
+                out=dst.bitcast(F32).rearrange("p (j r u) -> p j r u", j=TILES, u=2)[:, tiles],
+                in_=bank[:].rearrange("p (j u r) -> p j r u", j=TILES, u=2)[:, tiles],
             )
 
         def quantize_x(i):
-            nc.vector.quantize_mx(out=x_codes[i % 3][:].bitcast(FP8X4), scales=x_scales[i % 3][:], in_=xg[i % 2][:])
+            nc.vector.quantize_mx(out=x_codes[i % 3][:].bitcast(FP8X4), scales=x_scales[i % 3][:], in_=x_stage(i))
 
         def drive(i, b):
             z, g, u = seat(i), b // 2, b % 2
@@ -160,21 +172,30 @@ def tile_seatwise_crosstalk_canceller_k7_kernel(
                 func=ACT.Tanh,
             )
 
-        def apply_ceiling(i, g):
+        def d_part(tile, i, g, tiles):
+            if i == LAST:
+                return tile[:].rearrange("p a n -> p (a n)").rearrange("p (j g n) -> p j g n", j=TILES, g=PASSES)[
+                    :, tiles.start, g, :
+                ]
+            width = tile.shape[2] // TILES
+            return tile[:, g, tiles.start * width : tiles.stop * width]
+
+        def apply_ceiling(i, g, tiles):
             row = PASSES * seat(i) + g
+            count = (tiles.stop - tiles.start) * P
             ceil = ceil_ps[:].rearrange("p (u e r) -> p r u e", u=2, e=2)[:, row : row + 1, :, :]
             nc.vector.tensor_tensor(
-                out=d_bf[i % 2][:, g, :].rearrange("p (n u e) -> p n u e", u=2, e=2),
-                in0=th[(2 * i + g) % 4][:].rearrange("p u n e -> p n u e"),
-                in1=ceil.to_broadcast([P, GROUP, 2, 2]),
+                out=d_part(d_bf[i % 2], i, g, tiles).rearrange("p (n u e) -> p n u e", u=2, e=2),
+                in0=th[(2 * i + g) % 4][:].rearrange("p u n e -> p n u e")[:, tiles.start * P : tiles.stop * P],
+                in1=ceil.to_broadcast([P, count, 2, 2]),
                 op=ALU.mult,
             )
 
-        def quantize_d(i):
+        def quantize_d(i, halves):
             nc.vector.quantize_mx(
-                out=d_codes[i % 2][:].rearrange("p g n -> p (g n)").bitcast(FP8X4),
-                scales=d_scales[i % 2][:].rearrange("p g n -> p (g n)"),
-                in_=d_bf[i % 2][:].rearrange("p g n -> p (g n)"),
+                out=d_codes[i % 2][:, halves, :].rearrange("p a n -> p (a n)").bitcast(FP8X4),
+                scales=d_scales[i % 2][:, halves, :].rearrange("p a n -> p (a n)"),
+                in_=d_bf[i % 2][:, halves, :].rearrange("p a n -> p (a n)"),
             )
 
         def room(i, j):
@@ -182,8 +203,8 @@ def tile_seatwise_crosstalk_canceller_k7_kernel(
             for g in range(PASSES):
                 nc.tensor.matmul_mx(
                     out=v_ps[j][:],
-                    lhsT=d_codes[i % 2][:, g, j * P : (j + 1) * P].bitcast(FP8X4),
-                    lhsT_scale=d_scales[i % 2][:, g, j * P : (j + 1) * P],
+                    lhsT=d_part(d_codes[i % 2], i, g, slice(j, j + 1)).bitcast(FP8X4),
+                    lhsT_scale=d_part(d_scales[i % 2], i, g, slice(j, j + 1)),
                     rhs=h_sb[z][:, g, :].bitcast(FP4X4),
                     rhs_scale=hs_sb[:, PASSES * z + g, :],
                     start=(g == 0),
@@ -192,12 +213,20 @@ def tile_seatwise_crosstalk_canceller_k7_kernel(
 
         def add_bypass(i, j):
             nc.vector.tensor_tensor(
-                out=s_sb[(2 * i + j) % 3][:], in0=v_ps[j][:], in1=bypass_sb[i][:, j, :], op=ALU.add
+                out=s_sb[(2 * i + j) % 4][:], in0=v_ps[j][:], in1=bypass_sb[i][:, j, :], op=ALU.add
             )
 
-        def apply_gain(i, j):
-            nc.gpsimd.tensor_tensor(
-                out=y_sb[i][:, j, :], in0=s_sb[(2 * i + j) % 3][:], in1=gain_sb[seat(i)][:], op=ALU.mult
+        def apply_gain(engine, i, j):
+            engine.tensor_tensor(
+                out=y_sb[i][:, j, :], in0=s_sb[(2 * i + j) % 4][:], in1=gain_sb[seat(i)][:], op=ALU.mult
+            )
+
+        def apply_gain_rounded(i, j):
+            nc.vector.tensor_tensor(
+                out=y_bf[i % 2][:, j, :].rearrange("p (u m e) -> p u m e", u=2, e=2),
+                in0=s_sb[(2 * i + j) % 4][:].rearrange("p (m u e) -> p u m e", u=2, e=2),
+                in1=gain_sb[seat(i)][:].rearrange("p (m u e) -> p u m e", u=2, e=2),
+                op=ALU.mult,
             )
 
         def round_y(i, j):
@@ -206,141 +235,211 @@ def tile_seatwise_crosstalk_canceller_k7_kernel(
                 in_=y_sb[i][:, j, :].rearrange("p (m u e) -> p u m e", u=2, e=2),
             )
 
-        def turn_y(i):
-            for j in range(TILES):
-                words = y_bf[i % 2][:, j, :].bitcast(F32)
-                for u in range(2):
-                    col = (2 * j + u) * P
-                    nc.tensor.transpose(y_ps[:, col : col + P], words[:, u * P : (u + 1) * P], ident[:])
+        def turn_y(i, j, bank):
+            words = y_bf[i % 2][:, j, :].bitcast(F32)
+            for u in range(2):
+                col = (2 * j + u) * P
+                nc.tensor.transpose(bank[:, col : col + P], words[:, u * P : (u + 1) * P], ident[:])
 
-        def quantize_y(i):
-            cols = slice(i * GROUP, (i + 1) * GROUP)
-            nc.vector.quantize_mx(out=y_codes[:, cols].bitcast(FP8X4), scales=y_scales[:, cols], in_=yg[i % 2][:])
+        def frames(i, tiles):
+            return slice(i * GROUP + tiles.start * P, i * GROUP + tiles.stop * P)
 
-        def store_y(i):
-            nc.sync.dma_start(out=group_rows(y_rows, i), in_=y_sb[i][:])
+        def quantize_y(i, tiles):
+            cols = frames(i, tiles)
+            nc.vector.quantize_mx(
+                out=y_codes[:, cols].bitcast(FP8X4),
+                scales=y_scales[:, cols],
+                in_=y_stage(i)[:, tiles.start * 4 * P : tiles.stop * 4 * P],
+            )
 
-        def store_codes(i):
-            cols = slice(i * GROUP, (i + 1) * GROUP)
+        def store_y(i, tiles):
+            nc.sync.dma_start(out=group_rows(y_rows, i)[:, tiles, :], in_=y_sb[i][:, tiles, :])
+
+        def store_codes(cols):
             nc.sync.dma_start(out=y_words[:, cols], in_=y_codes[:, cols].bitcast(I32))
 
-        def store_scales(first, last):
-            cols = slice(first * GROUP, (last + 1) * GROUP)
+        def store_scales(engine, cols):
             for q in range(4):
-                nc.sync.dma_start(
+                engine.dma_start(
                     out=y_scale_rows[4 * q : 4 * q + 4, cols].bitcast(I32),
                     in_=y_scales[32 * q : 32 * q + 4, cols].bitcast(I32),
                 )
 
-        nc.vector.memset(cs_raw[:].bitcast(I32), 0)
+        nc.gpsimd.memset(cs_raw[:].bitcast(I32), 0)
+        make_identity(nc, ident[:])
         nc.vector.memset(warm[:], 0.0)
         nc.vector.memset(ceil_f32[:], 0.0)
-        make_identity(nc, ident[:])
-        nc.gpsimd.memset(hs_sb[:].rearrange("p g n -> p (g n)").bitcast(I32), 0)
+        nc.vector.memset(hs_sb[:].rearrange("p g n -> p (g n)").bitcast(I32), 0)
         for z in range(1, Z):
-            nc.gpsimd.memset(cs_sb[z][:].bitcast(I32), 0)
+            nc.vector.memset(cs_sb[z][:].bitcast(I32), 0)
 
+        load_c(slice(0, 1))
         load_x(0)
-        load_c(0)
+        nc.scalar.dma_start(
+            out=ceil_rows[0 : Z * PASSES, :], in_=ceiling.rearrange("z (g f) -> (z g) f", g=PASSES)
+        )
         for q in range(4):
             nc.scalar.dma_start(
                 out=cs_raw[32 * q : 32 * q + 16, :].bitcast(I32),
                 in_=c_scales[:, 4 * q : 4 * q + 4, :].bitcast(I32),
             )
         nc.scalar.activation(out=warm[:], in_=warm[:], func=ACT.Tanh)
-        nc.sync.dma_start(
-            out=ceil_rows[0 : Z * PASSES, :], in_=ceiling.rearrange("z (g f) -> (z g) f", g=PASSES)
-        )
         load_x(1)
+        load_c(slice(1, 2))
+        load_c(slice(2, 3))
         load_x(2)
-        load_c(1)
+        load_c(slice(3, 4))
         for q in range(4):
             nc.sync.dma_start(
                 out=hs_sb[32 * q : 32 * q + 4, :, :].bitcast(I32),
                 in_=h_scales[:, 4 * q : 4 * q + 4, :].rearrange("g r n -> r g n").bitcast(I32),
             )
-        load_h(0)
         load_x(3)
+        load_h(0)
         load_bypass(0)
         load_gain(0)
+        load_x(4)
+        load_bypass(1)
 
-        permute_c_scales(0)
+        nc.scalar.copy(out=ceil_f32[0 : Z * PASSES, :], in_=ceil_rows[0 : Z * PASSES, :])
+        turn_x(0, x_ps)
+        gather_words(x_stage(0), x_ps, BOTH)
+        for t in range(4):
+            nc.tensor.transpose(ceil_ps[:, t * P : (t + 1) * P], ceil_f32[:, t : 512 : 4], ident[:])
         permute_c(0, 0)
-        nc.vector.tensor_copy(out=ceil_f32[0 : Z * PASSES, :], in_=ceil_rows[0 : Z * PASSES, :])
+        permute_c(0, 1)
+        permute_c_scales(0)
+        permute_c_scales(1)
+        quantize_x(0)
+        drive(0, 0)
+        drive(0, 1)
+        turn_x(1, y_ps)
+        drive(0, 2)
+        permute_c(1, 0)
+        permute_c(1, 1)
+        permute_c(2, 0)
+        permute_c(2, 1)
+        limit(0, 0)
+        limit(0, 1)
+        drive(0, 3)
+        gather_words(x_stage(1), y_ps, BOTH)
+        limit(0, 2)
+        turn_x(2, x_ps)
+        for z in range(1, Z):
+            shift_c_scales(z)
 
         def live(i):
             return 0 <= i < GROUPS
 
-        for k in range(-3, GROUPS + 3):
+        for k in range(LAST):
+            apply_ceiling(k, 0, BOTH)
+            if k == 0:
+                quantize_x(1)
+                permute_c(3, 0)
             if live(k - 2):
-                add_bypass(k - 2, 0)
-            if live(k - 3):
-                gather_words(yg[(k - 3) % 2], y_ps)
-            if live(k + 1):
-                for b in range(3):
-                    drive(k + 1, b)
-            if live(k - 2):
-                add_bypass(k - 2, 1)
-                apply_gain(k - 2, 0)
-            if live(k + 2):
-                gather_words(xg[(k + 2) % 2], x_ps)
+                apply_gain(nc.gpsimd, k - 2, 1)
+                store_y(k - 2, BOTH)
+            limit(k, 3)
             if live(k - 1):
                 room(k - 1, 0)
-            if live(k):
-                apply_ceiling(k, 0)
-            if live(k - 2):
-                apply_gain(k - 2, 1)
-                store_y(k - 2)
-            if live(k + 1):
-                limit(k + 1, 0)
-                limit(k + 1, 1)
-            if live(k + 3):
-                turn_x(k + 3)
-            if k == -2:
-                for t in range(4):
-                    nc.tensor.transpose(ceil_ps[:, t * P : (t + 1) * P], ceil_f32[:, t : 512 : 4], ident[:])
-            if live(k):
-                apply_ceiling(k, 1)
-            if live(k - 2):
-                round_y(k - 2, 0)
-            if live(k + 1):
-                drive(k + 1, 3)
-            if live(k - 1):
                 room(k - 1, 1)
             if live(k + 1):
-                limit(k + 1, 2)
-            if live(k - 3):
-                quantize_y(k - 3)
-                store_codes(k - 3)
+                drive(k + 1, 0)
+                drive(k + 1, 1)
             if live(k + 2):
-                quantize_x(k + 2)
-            if k == -2:
-                permute_c_scales(1)
-                permute_c(0, 1)
-            if k == -1:
-                permute_c(1, 0)
-                permute_c(1, 1)
-                for z in range(1, Z):
-                    shift_c_scales(z)
-            if k in (1, 2, 4, 5):
-                permute_c(2 + k // 4, (k - 1) % 3)
-            if live(k):
-                quantize_d(k)
+                gather_words(x_stage(k + 2), x_ps, BOTH)
+            if live(k - 3):
+                gather_words(y_stage(k - 3), y_ps, BOTH)
+            if live(k - 1):
+                add_bypass(k - 1, 0)
+            if live(k + 3):
+                turn_x(k + 3, x_ps)
+            if live(k + 1):
+                drive(k + 1, 2)
+                limit(k + 1, 0)
+                drive(k + 1, 3)
+                limit(k + 1, 1)
+            apply_ceiling(k, 1, BOTH)
+            if live(k - 1):
+                apply_gain(nc.gpsimd, k - 1, 0)
             if live(k - 2):
                 round_y(k - 2, 1)
+                turn_y(k - 2, 0, y_ps)
+                turn_y(k - 2, 1, y_ps)
             if live(k + 1):
+                limit(k + 1, 2)
+            if k + 1 == LAST:
                 limit(k + 1, 3)
-            if live(k - 2):
-                turn_y(k - 2)
-            if live(k + 5) and k + 5 > 3:
+            if live(k - 1):
+                add_bypass(k - 1, 1)
+            if live(k + 2) and k not in (1, 2):
+                quantize_x(k + 2)
+            quantize_d(k, BOTH)
+            if k == 0:
+                permute_c(3, 1)
+            if k in (1, 2):
+                quantize_x(k + 2)
+            if live(k - 3):
+                quantize_y(k - 3, BOTH)
+                store_codes(frames(k - 3, BOTH))
+            if k + 1 == LAST:
+                store_scales(nc.sync, slice(0, (k - 2) * GROUP))
+            if live(k - 1):
+                round_y(k - 1, 0)
+            if live(k + 5):
                 load_x(k + 5)
-            if live(k + 2) and k + 2 > 0:
+            if live(k + 2):
                 load_bypass(k + 2)
-            if k in (-1, 2):
-                load_c(2 + k // 2 if k > 0 else 2)
             if k in (0, 3, 6):
                 load_h(k // 3 + 1)
                 load_gain(k // 3 + 1)
-            if k - 3 == GROUPS - 3:
-                store_scales(0, GROUPS - 3)
-        store_scales(GROUPS - 2, GROUPS - 1)
+
+        a, b, c, d = LAST - 3, LAST - 2, LAST - 1, LAST
+        room(c, 0)
+        room(c, 1)
+        apply_ceiling(d, 0, TILE0)
+        apply_gain(nc.gpsimd, b, 1)
+        store_y(b, BOTH)
+        gather_words(y_stage(a), y_ps, BOTH)
+        apply_ceiling(d, 1, TILE0)
+        add_bypass(c, 0)
+        quantize_d(d, TILE0)
+        room(d, 0)
+        apply_gain(nc.gpsimd, c, 0)
+        round_y(b, 1)
+        turn_y(b, 0, y_ps)
+        turn_y(b, 1, y_ps)
+        apply_ceiling(d, 0, TILE1)
+        apply_ceiling(d, 1, TILE1)
+        add_bypass(c, 1)
+        quantize_d(d, TILE1)
+        room(d, 1)
+        gather_words(y_stage(b), y_ps, BOTH)
+        round_y(c, 0)
+        add_bypass(d, 0)
+        apply_gain(nc.vector, c, 1)
+        store_y(c, BOTH)
+        round_y(c, 1)
+        turn_y(c, 0, y_ps)
+        turn_y(c, 1, y_ps)
+        apply_gain(nc.vector, d, 0)
+        store_y(d, TILE0)
+        round_y(d, 0)
+        turn_y(d, 0, x_ps)
+        add_bypass(d, 1)
+        quantize_y(a, BOTH)
+        store_codes(frames(a, BOTH))
+        gather_words(y_stage(c), y_ps, BOTH)
+        gather_words(y_stage(d), x_ps, TILE0)
+        apply_gain_rounded(d, 1)
+        turn_y(d, 1, u_ps[0])
+        apply_gain(nc.vector, d, 1)
+        store_y(d, TILE1)
+        gather_words(y_stage(d), u_ps[0], TILE1)
+        quantize_y(b, BOTH)
+        quantize_y(c, BOTH)
+        quantize_y(d, TILE0)
+        store_codes(slice(b * GROUP, d * GROUP + P))
+        quantize_y(d, TILE1)
+        store_codes(frames(d, TILE1))
+        store_scales(nc.scalar, slice(a * GROUP, (d + 1) * GROUP))

@@ -28,6 +28,7 @@ LAST = GROUPS - 1
 BOTH = slice(0, TILES)
 TILE0 = slice(0, 1)
 TILE1 = slice(1, 2)
+ALL_WORDS = slice(0, P)
 
 
 def tile_seatwise_crosstalk_canceller_k7_kernel(
@@ -63,13 +64,13 @@ def tile_seatwise_crosstalk_canceller_k7_kernel(
         ceil_rows = sb.tile([P, 512], BF16, name="ceil_rows", align_bytes=64)
         ceil_f32 = sb.tile([P, 512], F32, name="ceil_f32", align_bytes=64)
         xg = ring("xg", 2, [P, GROUP * 4], BF16)
-        x_codes = ring("x_codes", 3, [P, GROUP], U32)
-        x_scales = ring("x_scales", 3, [P, GROUP], U8)
-        th = ring("th", 4, [P, 2, GROUP, 2], F32)
+        x_codes = ring("x_codes", 4, [P, GROUP], U32)
+        x_scales = ring("x_scales", 4, [P, GROUP], U8)
+        th = ring("th", 2, [P, 2, PASSES, GROUP, 2], F32)
         d_bf = ring("d_bf", 2, [P, PASSES, GROUP * 4], BF16)
         d_codes = ring("d_codes", 2, [P, PASSES, GROUP], U32)
         d_scales = ring("d_scales", 2, [P, PASSES, GROUP], U8)
-        s_sb = ring("s", 4, [P, E], F32)
+        s_sb = ring("s", 2, [P, TILES, E], F32)
         y_bf = ring("y_bf", 2, [P, TILES, E], BF16)
         yg = ring("yg", 4, [P, GROUP * 4], BF16)
         y_codes = sb.tile([P, Z * R], U32, name="y_codes", align_bytes=64)
@@ -81,11 +82,15 @@ def tile_seatwise_crosstalk_canceller_k7_kernel(
         u_ps = [ps.tile([P, 512], F32, name="u_ps%d" % i) for i in range(DRIVE_BANKS)]
         v_ps = [ps.tile([P, 512], F32, name="v_ps%d" % i) for i in range(TILES)]
 
-        def x_stage(i):
-            return y_sb[i - 3][:, 1, :].bitcast(BF16) if i in (3, 4) else xg[i % 2][:]
+        def d_stage(i):
+            if i in (1, LAST - 1, LAST):
+                return y_sb[i - 1][:].bitcast(BF16)
+            return d_bf[i % 2][:]
 
-        def y_stage(i):
-            return y_sb[i + 2][:, 1, :].bitcast(BF16) if i < LAST - 3 else yg[i % 4][:]
+        def y_rounded(i, j):
+            if j == 1 and i < LAST - 3:
+                return d_stage(i + 2)[:, 0, 0:E]
+            return y_bf[i % 2][:, j, :]
 
         def seat(i):
             return i // GROUPS_PER_SEAT
@@ -147,7 +152,7 @@ def tile_seatwise_crosstalk_canceller_k7_kernel(
             )
 
         def quantize_x(i):
-            nc.vector.quantize_mx(out=x_codes[i % 3][:].bitcast(FP8X4), scales=x_scales[i % 3][:], in_=x_stage(i))
+            nc.vector.quantize_mx(out=x_codes[i % 4][:].bitcast(FP8X4), scales=x_scales[i % 4][:], in_=xg[i % 2][:])
 
         def drive(i, b):
             z, g, u = seat(i), b // 2, b % 2
@@ -158,8 +163,8 @@ def tile_seatwise_crosstalk_canceller_k7_kernel(
                     out=bank[:, e * GROUP : (e + 1) * GROUP],
                     lhsT=c_sb[z][:, 2 * col : 2 * (col + P)].bitcast(FP4X4),
                     lhsT_scale=cs_sb[z][:, col : col + P],
-                    rhs=x_codes[i % 3][:].bitcast(FP8X4),
-                    rhs_scale=x_scales[i % 3][:],
+                    rhs=x_codes[i % 4][:].bitcast(FP8X4),
+                    rhs_scale=x_scales[i % 4][:],
                     start=True,
                     stop=True,
                 )
@@ -167,27 +172,34 @@ def tile_seatwise_crosstalk_canceller_k7_kernel(
         def limit(i, b):
             bank = u_ps[(4 * i + b) % DRIVE_BANKS]
             nc.scalar.activation(
-                out=th[(2 * i + b // 2) % 4][:, b % 2, :, :],
+                out=th[i % 2][:, b % 2, b // 2, :, :],
                 in_=bank[:].rearrange("p (e n) -> p n e", e=2),
                 func=ACT.Tanh,
             )
 
-        def d_part(tile, i, g, tiles):
+        def d_part(ap, i, g, j):
+            width = ap.shape[2] // TILES
             if i == LAST:
-                return tile[:].rearrange("p a n -> p (a n)").rearrange("p (j g n) -> p j g n", j=TILES, g=PASSES)[
-                    :, tiles.start, g, :
-                ]
-            width = tile.shape[2] // TILES
-            return tile[:, g, tiles.start * width : tiles.stop * width]
+                return ap[:, j, g * width : (g + 1) * width]
+            return ap[:, g, j * width : (j + 1) * width]
 
-        def apply_ceiling(i, g, tiles):
+        def apply_ceiling(i):
+            rows = slice(PASSES * seat(i), PASSES * (seat(i) + 1))
+            ceil = ceil_ps[:].rearrange("p (t r n) -> p r n t", t=4, n=1)[:, rows, :, :]
+            nc.vector.tensor_tensor(
+                out=d_stage(i).rearrange("p g (n t) -> p g n t", t=4),
+                in0=th[i % 2][:].rearrange("p u g n e -> p (g n) u e"),
+                in1=ceil.to_broadcast([P, PASSES, GROUP, 4]),
+                op=ALU.mult,
+            )
+
+        def apply_ceiling_part(i, g, j):
             row = PASSES * seat(i) + g
-            count = (tiles.stop - tiles.start) * P
             ceil = ceil_ps[:].rearrange("p (u e r) -> p r u e", u=2, e=2)[:, row : row + 1, :, :]
             nc.vector.tensor_tensor(
-                out=d_part(d_bf[i % 2], i, g, tiles).rearrange("p (n u e) -> p n u e", u=2, e=2),
-                in0=th[(2 * i + g) % 4][:].rearrange("p u n e -> p n u e")[:, tiles.start * P : tiles.stop * P],
-                in1=ceil.to_broadcast([P, count, 2, 2]),
+                out=d_part(d_stage(i), i, g, j).rearrange("p (n u e) -> p n u e", u=2, e=2),
+                in0=th[i % 2][:, :, g, j * P : (j + 1) * P, :].rearrange("p u n e -> p n u e"),
+                in1=ceil.to_broadcast([P, P, 2, 2]),
                 op=ALU.mult,
             )
 
@@ -195,16 +207,19 @@ def tile_seatwise_crosstalk_canceller_k7_kernel(
             nc.vector.quantize_mx(
                 out=d_codes[i % 2][:, halves, :].rearrange("p a n -> p (a n)").bitcast(FP8X4),
                 scales=d_scales[i % 2][:, halves, :].rearrange("p a n -> p (a n)"),
-                in_=d_bf[i % 2][:, halves, :].rearrange("p a n -> p (a n)"),
+                in_=d_stage(i)[:, halves, :].rearrange("p a n -> p (a n)"),
             )
+
+        def ear_bank(i, j):
+            return u_ps[1] if (i, j) == (LAST, 1) else v_ps[j]
 
         def room(i, j):
             z = seat(i)
             for g in range(PASSES):
                 nc.tensor.matmul_mx(
-                    out=v_ps[j][:],
-                    lhsT=d_part(d_codes[i % 2], i, g, slice(j, j + 1)).bitcast(FP8X4),
-                    lhsT_scale=d_part(d_scales[i % 2], i, g, slice(j, j + 1)),
+                    out=ear_bank(i, j)[:],
+                    lhsT=d_part(d_codes[i % 2][:], i, g, j).bitcast(FP8X4),
+                    lhsT_scale=d_part(d_scales[i % 2][:], i, g, j),
                     rhs=h_sb[z][:, g, :].bitcast(FP4X4),
                     rhs_scale=hs_sb[:, PASSES * z + g, :],
                     start=(g == 0),
@@ -213,30 +228,47 @@ def tile_seatwise_crosstalk_canceller_k7_kernel(
 
         def add_bypass(i, j):
             nc.vector.tensor_tensor(
-                out=s_sb[(2 * i + j) % 4][:], in0=v_ps[j][:], in1=bypass_sb[i][:, j, :], op=ALU.add
+                out=s_sb[i % 2][:, j, :], in0=ear_bank(i, j)[:], in1=bypass_sb[i][:, j, :], op=ALU.add
             )
 
-        def apply_gain(engine, i, j):
+        def apply_gain(engine, i, tiles):
+            count = tiles.stop - tiles.start
             engine.tensor_tensor(
-                out=y_sb[i][:, j, :], in0=s_sb[(2 * i + j) % 4][:], in1=gain_sb[seat(i)][:], op=ALU.mult
-            )
-
-        def apply_gain_rounded(i, j):
-            nc.vector.tensor_tensor(
-                out=y_bf[i % 2][:, j, :].rearrange("p (u m e) -> p u m e", u=2, e=2),
-                in0=s_sb[(2 * i + j) % 4][:].rearrange("p (m u e) -> p u m e", u=2, e=2),
-                in1=gain_sb[seat(i)][:].rearrange("p (m u e) -> p u m e", u=2, e=2),
+                out=y_sb[i][:, tiles, :],
+                in0=s_sb[i % 2][:, tiles, :],
+                in1=gain_sb[seat(i)][:].rearrange("p (j e) -> p j e", j=1).to_broadcast([P, count, E]),
                 op=ALU.mult,
             )
 
-        def round_y(i, j):
-            nc.scalar.copy(
-                out=y_bf[i % 2][:, j, :].rearrange("p (u m e) -> p u m e", u=2, e=2),
-                in_=y_sb[i][:, j, :].rearrange("p (m u e) -> p u m e", u=2, e=2),
+        def by_word_half(ap):
+            return ap.rearrange("p (m u e) -> p u m e", u=2, e=2)
+
+        def rounded(i, j):
+            return y_rounded(i, j).rearrange("p (u m e) -> p u m e", u=2, e=2)
+
+        def apply_gain_rounded(i, j):
+            nc.vector.tensor_tensor(
+                out=rounded(i, j),
+                in0=by_word_half(s_sb[i % 2][:, j, :]),
+                in1=by_word_half(gain_sb[seat(i)][:]),
+                op=ALU.mult,
+            )
+
+        def round_y(i, j, words):
+            nc.scalar.copy(out=rounded(i, j)[:, :, words, :], in_=by_word_half(y_sb[i][:, j, :])[:, :, words, :])
+
+        def round_y_gpsimd(i, j, words):
+            nc.gpsimd.tensor_scalar(
+                out=rounded(i, j)[:, :, words, :],
+                in0=by_word_half(y_sb[i][:, j, :])[:, :, words, :],
+                scalar1=1.0,
+                scalar2=-0.0,
+                op0=ALU.mult,
+                op1=ALU.add,
             )
 
         def turn_y(i, j, bank):
-            words = y_bf[i % 2][:, j, :].bitcast(F32)
+            words = y_rounded(i, j).bitcast(F32)
             for u in range(2):
                 col = (2 * j + u) * P
                 nc.tensor.transpose(bank[:, col : col + P], words[:, u * P : (u + 1) * P], ident[:])
@@ -249,7 +281,7 @@ def tile_seatwise_crosstalk_canceller_k7_kernel(
             nc.vector.quantize_mx(
                 out=y_codes[:, cols].bitcast(FP8X4),
                 scales=y_scales[:, cols],
-                in_=y_stage(i)[:, tiles.start * 4 * P : tiles.stop * 4 * P],
+                in_=yg[i % 4][:, tiles.start * 4 * P : tiles.stop * 4 * P],
             )
 
         def store_y(i, tiles):
@@ -289,23 +321,24 @@ def tile_seatwise_crosstalk_canceller_k7_kernel(
         load_c(slice(2, 3))
         load_x(2)
         load_c(slice(3, 4))
+        load_x(3)
         for q in range(4):
             nc.sync.dma_start(
                 out=hs_sb[32 * q : 32 * q + 4, :, :].bitcast(I32),
                 in_=h_scales[:, 4 * q : 4 * q + 4, :].rearrange("g r n -> r g n").bitcast(I32),
             )
-        load_x(3)
         load_h(0)
+        load_x(4)
         load_bypass(0)
         load_gain(0)
-        load_x(4)
+        load_x(5)
         load_bypass(1)
 
         nc.scalar.copy(out=ceil_f32[0 : Z * PASSES, :], in_=ceil_rows[0 : Z * PASSES, :])
         turn_x(0, x_ps)
-        gather_words(x_stage(0), x_ps, BOTH)
-        for t in range(4):
-            nc.tensor.transpose(ceil_ps[:, t * P : (t + 1) * P], ceil_f32[:, t : 512 : 4], ident[:])
+        turn_x(1, y_ps)
+        gather_words(xg[0][:], x_ps, BOTH)
+        gather_words(xg[1][:], y_ps, BOTH)
         permute_c(0, 0)
         permute_c(0, 1)
         permute_c_scales(0)
@@ -313,133 +346,150 @@ def tile_seatwise_crosstalk_canceller_k7_kernel(
         quantize_x(0)
         drive(0, 0)
         drive(0, 1)
-        turn_x(1, y_ps)
         drive(0, 2)
         permute_c(1, 0)
+        quantize_x(1)
         permute_c(1, 1)
         permute_c(2, 0)
         permute_c(2, 1)
+        permute_c(3, 0)
         limit(0, 0)
-        limit(0, 1)
         drive(0, 3)
-        gather_words(x_stage(1), y_ps, BOTH)
+        for t in range(4):
+            nc.tensor.transpose(ceil_ps[:, t * P : (t + 1) * P], ceil_f32[:, t : 512 : 4], ident[:])
+        limit(0, 1)
         limit(0, 2)
+        drive(1, 0)
+        drive(1, 1)
         turn_x(2, x_ps)
+        turn_x(3, y_ps)
+        limit(0, 3)
+        drive(1, 2)
         for z in range(1, Z):
             shift_c_scales(z)
+        apply_ceiling(0)
+        limit(1, 0)
+        drive(1, 3)
+        gather_words(xg[0][:], x_ps, BOTH)
+        turn_x(4, x_ps)
+        limit(1, 1)
+        limit(1, 2)
+        quantize_x(2)
+        limit(1, 3)
+        drive(2, 0)
+        drive(2, 1)
+        gather_words(xg[1][:], y_ps, BOTH)
+        quantize_d(0, BOTH)
+        permute_c(3, 1)
+        load_x(6)
+        load_bypass(2)
+        load_h(1)
+        load_gain(1)
 
         def live(i):
             return 0 <= i < GROUPS
 
-        for k in range(LAST):
-            apply_ceiling(k, 0, BOTH)
-            if k == 0:
-                quantize_x(1)
-                permute_c(3, 0)
+        for k in range(1, LAST):
+            apply_ceiling(k)
+            if k == 1:
+                quantize_x(3)
+            if live(k - 3):
+                round_y_gpsimd(k - 3, 1, ALL_WORDS)
             if live(k - 2):
-                apply_gain(nc.gpsimd, k - 2, 1)
+                apply_gain(nc.gpsimd, k - 2, BOTH)
                 store_y(k - 2, BOTH)
-            limit(k, 3)
+            if live(k + 3):
+                gather_words(xg[(k + 3) % 2][:], x_ps, BOTH)
+            limit(k + 1, 0)
+            limit(k + 1, 1)
             if live(k - 1):
                 room(k - 1, 0)
-                room(k - 1, 1)
-            if live(k + 1):
-                drive(k + 1, 0)
-                drive(k + 1, 1)
-            if live(k + 2):
-                gather_words(x_stage(k + 2), x_ps, BOTH)
+            drive(k + 1, 2)
             if live(k - 3):
-                gather_words(y_stage(k - 3), y_ps, BOTH)
+                turn_y(k - 3, 0, y_ps)
+                turn_y(k - 3, 1, y_ps)
+                gather_words(yg[(k - 3) % 4][:], y_ps, BOTH)
+            if live(k - 1):
+                room(k - 1, 1)
+            drive(k + 1, 3)
+            if live(k + 4):
+                turn_x(k + 4, x_ps)
+            limit(k + 1, 2)
+            limit(k + 1, 3)
             if live(k - 1):
                 add_bypass(k - 1, 0)
-            if live(k + 3):
-                turn_x(k + 3, x_ps)
-            if live(k + 1):
-                drive(k + 1, 2)
-                limit(k + 1, 0)
-                drive(k + 1, 3)
-                limit(k + 1, 1)
-            apply_ceiling(k, 1, BOTH)
-            if live(k - 1):
-                apply_gain(nc.gpsimd, k - 1, 0)
-            if live(k - 2):
-                round_y(k - 2, 1)
-                turn_y(k - 2, 0, y_ps)
-                turn_y(k - 2, 1, y_ps)
-            if live(k + 1):
-                limit(k + 1, 2)
-            if k + 1 == LAST:
-                limit(k + 1, 3)
-            if live(k - 1):
                 add_bypass(k - 1, 1)
-            if live(k + 2) and k not in (1, 2):
-                quantize_x(k + 2)
+            if live(k + 2):
+                drive(k + 2, 0)
+                drive(k + 2, 1)
+            if live(k + 3) and k >= 3:
+                quantize_x(k + 3)
             quantize_d(k, BOTH)
-            if k == 0:
-                permute_c(3, 1)
-            if k in (1, 2):
-                quantize_x(k + 2)
+            if k < 3:
+                quantize_x(k + 3)
             if live(k - 3):
                 quantize_y(k - 3, BOTH)
                 store_codes(frames(k - 3, BOTH))
             if k + 1 == LAST:
                 store_scales(nc.sync, slice(0, (k - 2) * GROUP))
-            if live(k - 1):
-                round_y(k - 1, 0)
-            if live(k + 5):
-                load_x(k + 5)
+            if live(k - 2):
+                round_y(k - 2, 0, ALL_WORDS)
+            if k + 1 == LAST:
+                round_y(k - 2, 1, ALL_WORDS)
+            if live(k + 6):
+                load_x(k + 6)
             if live(k + 2):
                 load_bypass(k + 2)
-            if k in (0, 3, 6):
+            if k in (3, 6):
                 load_h(k // 3 + 1)
                 load_gain(k // 3 + 1)
 
         a, b, c, d = LAST - 3, LAST - 2, LAST - 1, LAST
         room(c, 0)
+        turn_y(a, 0, y_ps)
+        turn_y(a, 1, y_ps)
         room(c, 1)
-        apply_ceiling(d, 0, TILE0)
-        apply_gain(nc.gpsimd, b, 1)
+        apply_ceiling_part(d, 0, 0)
+        apply_gain(nc.gpsimd, b, BOTH)
         store_y(b, BOTH)
-        gather_words(y_stage(a), y_ps, BOTH)
-        apply_ceiling(d, 1, TILE0)
+        gather_words(yg[a % 4][:], y_ps, BOTH)
+        apply_ceiling_part(d, 1, 0)
+        apply_ceiling_part(d, 0, 1)
+        apply_ceiling_part(d, 1, 1)
         add_bypass(c, 0)
         quantize_d(d, TILE0)
+        quantize_d(d, TILE1)
         room(d, 0)
-        apply_gain(nc.gpsimd, c, 0)
-        round_y(b, 1)
+        room(d, 1)
+        round_y(b, 0, ALL_WORDS)
+        round_y(b, 1, ALL_WORDS)
         turn_y(b, 0, y_ps)
         turn_y(b, 1, y_ps)
-        apply_ceiling(d, 0, TILE1)
-        apply_ceiling(d, 1, TILE1)
+        apply_gain(nc.gpsimd, c, TILE0)
         add_bypass(c, 1)
-        quantize_d(d, TILE1)
-        room(d, 1)
-        gather_words(y_stage(b), y_ps, BOTH)
-        round_y(c, 0)
         add_bypass(d, 0)
-        apply_gain(nc.vector, c, 1)
+        add_bypass(d, 1)
+        round_y(c, 0, ALL_WORDS)
+        gather_words(yg[b % 4][:], y_ps, BOTH)
+        apply_gain(nc.vector, c, TILE1)
         store_y(c, BOTH)
-        round_y(c, 1)
+        round_y(c, 1, ALL_WORDS)
         turn_y(c, 0, y_ps)
         turn_y(c, 1, y_ps)
-        apply_gain(nc.vector, d, 0)
+        apply_gain(nc.vector, d, TILE0)
         store_y(d, TILE0)
-        round_y(d, 0)
-        turn_y(d, 0, x_ps)
-        add_bypass(d, 1)
-        quantize_y(a, BOTH)
-        store_codes(frames(a, BOTH))
-        gather_words(y_stage(c), y_ps, BOTH)
-        gather_words(y_stage(d), x_ps, TILE0)
+        round_y(d, 0, ALL_WORDS)
         apply_gain_rounded(d, 1)
-        turn_y(d, 1, u_ps[0])
-        apply_gain(nc.vector, d, 1)
+        turn_y(d, 1, x_ps)
+        turn_y(d, 0, x_ps)
+        gather_words(yg[c % 4][:], y_ps, BOTH)
+        apply_gain(nc.vector, d, TILE1)
         store_y(d, TILE1)
-        gather_words(y_stage(d), u_ps[0], TILE1)
+        gather_words(yg[d % 4][:], x_ps, BOTH)
+        quantize_y(a, BOTH)
         quantize_y(b, BOTH)
+        store_codes(slice(a * GROUP, c * GROUP))
         quantize_y(c, BOTH)
-        quantize_y(d, TILE0)
-        store_codes(slice(b * GROUP, d * GROUP + P))
-        quantize_y(d, TILE1)
-        store_codes(frames(d, TILE1))
+        quantize_y(d, BOTH)
+        store_codes(slice(c * GROUP, (d + 1) * GROUP))
         store_scales(nc.scalar, slice(a * GROUP, (d + 1) * GROUP))

@@ -28,7 +28,8 @@ LAST = GROUPS - 1
 BOTH = slice(0, TILES)
 TILE0 = slice(0, 1)
 TILE1 = slice(1, 2)
-ALL_WORDS = slice(0, P)
+LOW = slice(0, 1)
+HIGH = slice(1, 2)
 
 
 def tile_seatwise_crosstalk_canceller_k7_kernel(
@@ -57,12 +58,13 @@ def tile_seatwise_crosstalk_canceller_k7_kernel(
         c_raw = sb.tile([P, Z, 2 * F], U8, name="c_raw", align_bytes=64)
         c_sb = ring("c", Z, [P, 2 * F], U8)
         cs_raw = sb.tile([P, F], U8, name="cs_raw", align_bytes=64)
-        cs_sb = ring("cs", Z, [P, F], U8)
+        cs_first = sb.tile([P, F], U8, name="cs_first", align_bytes=64)
+        cs_sb = [cs_first[:], c_raw[:, 0, 0:F], c_raw[:, 0, F : 2 * F], cs_raw[:]]
         h_sb = ring("h", Z, [P, PASSES, 2 * E], U8)
         hs_sb = sb.tile([P, Z * PASSES, E], U8, name="hs", align_bytes=64)
         gain_sb = ring("gain", Z, [P, E], BF16)
         ceil_rows = sb.tile([P, 512], BF16, name="ceil_rows", align_bytes=64)
-        ceil_f32 = sb.tile([P, 512], F32, name="ceil_f32", align_bytes=64)
+        ceil_f32 = x_sb[0][:].rearrange("p j e -> p (j e)").bitcast(F32)
         xg = ring("xg", 2, [P, GROUP * 4], BF16)
         x_codes = ring("x_codes", 4, [P, GROUP], U32)
         x_scales = ring("x_scales", 4, [P, GROUP], U8)
@@ -87,10 +89,10 @@ def tile_seatwise_crosstalk_canceller_k7_kernel(
                 return y_sb[i - 1][:].bitcast(BF16)
             return d_bf[i % 2][:]
 
-        def y_rounded(i, j):
-            if j == 1 and i < LAST - 3:
-                return d_stage(i + 2)[:, 0, 0:E]
-            return y_bf[i % 2][:, j, :]
+        def y_rounded(i, j, halves):
+            if j == 1 and halves == HIGH and i < LAST - 3:
+                return d_stage(i + 2)[:, 0, 0 : E // 2]
+            return y_bf[i % 2][:, j, halves.start * (E // 2) : halves.stop * (E // 2)]
 
         def seat(i):
             return i // GROUPS_PER_SEAT
@@ -124,18 +126,16 @@ def tile_seatwise_crosstalk_canceller_k7_kernel(
                 in_=cs_sb[0][4 * z : 4 * z + SHIFT_ROWS, :].bitcast(I32),
             )
 
-        def permute_c(z, g):
-            cols = slice(g * 1024, (g + 1) * 1024)
+        def permute_c(z):
             nc.vector.tensor_copy(
-                out=c_sb[z][:, cols].rearrange("p (t m b) -> p t m b", t=4, b=2),
-                in_=c_raw[:, z, cols].rearrange("p (m t b) -> p t m b", t=4, b=2),
+                out=c_sb[z][:].rearrange("p (g t m b) -> p g t m b", g=PASSES, t=4, b=2),
+                in_=c_raw[:, z, :].rearrange("p (g m t b) -> p g t m b", g=PASSES, t=4, b=2),
             )
 
-        def permute_c_scales(g):
-            cols = slice(g * 512, (g + 1) * 512)
+        def permute_c_scales():
             nc.vector.tensor_copy(
-                out=cs_sb[0][:, cols].rearrange("p (t m) -> p t m", t=4),
-                in_=cs_raw[:, cols].rearrange("p (m t) -> p t m", t=4),
+                out=cs_sb[0].rearrange("p (g t m) -> p g t m", g=PASSES, t=4),
+                in_=cs_raw[:].rearrange("p (g m t) -> p g t m", g=PASSES, t=4),
             )
 
         def turn_x(i, bank):
@@ -185,7 +185,7 @@ def tile_seatwise_crosstalk_canceller_k7_kernel(
 
         def apply_ceiling(i):
             rows = slice(PASSES * seat(i), PASSES * (seat(i) + 1))
-            ceil = ceil_ps[:].rearrange("p (t r n) -> p r n t", t=4, n=1)[:, rows, :, :]
+            ceil = ceil_ps[:].rearrange("p (r n t) -> p r n t", t=4, n=1)[:, rows, :, :]
             nc.vector.tensor_tensor(
                 out=d_stage(i).rearrange("p g (n t) -> p g n t", t=4),
                 in0=th[i % 2][:].rearrange("p u g n e -> p (g n) u e"),
@@ -195,7 +195,7 @@ def tile_seatwise_crosstalk_canceller_k7_kernel(
 
         def apply_ceiling_part(i, g, j):
             row = PASSES * seat(i) + g
-            ceil = ceil_ps[:].rearrange("p (u e r) -> p r u e", u=2, e=2)[:, row : row + 1, :, :]
+            ceil = ceil_ps[:].rearrange("p (r u e) -> p r u e", u=2, e=2)[:, row : row + 1, :, :]
             nc.vector.tensor_tensor(
                 out=d_part(d_stage(i), i, g, j).rearrange("p (n u e) -> p n u e", u=2, e=2),
                 in0=th[i % 2][:, :, g, j * P : (j + 1) * P, :].rearrange("p u n e -> p n u e"),
@@ -243,24 +243,24 @@ def tile_seatwise_crosstalk_canceller_k7_kernel(
         def by_word_half(ap):
             return ap.rearrange("p (m u e) -> p u m e", u=2, e=2)
 
-        def rounded(i, j):
-            return y_rounded(i, j).rearrange("p (u m e) -> p u m e", u=2, e=2)
+        def rounded(i, j, halves):
+            return y_rounded(i, j, halves).rearrange("p (u m e) -> p u m e", m=P, e=2)
 
         def apply_gain_rounded(i, j):
             nc.vector.tensor_tensor(
-                out=rounded(i, j),
+                out=rounded(i, j, BOTH),
                 in0=by_word_half(s_sb[i % 2][:, j, :]),
                 in1=by_word_half(gain_sb[seat(i)][:]),
                 op=ALU.mult,
             )
 
-        def round_y(i, j, words):
-            nc.scalar.copy(out=rounded(i, j)[:, :, words, :], in_=by_word_half(y_sb[i][:, j, :])[:, :, words, :])
+        def round_y(i, j, halves):
+            nc.scalar.copy(out=rounded(i, j, halves), in_=by_word_half(y_sb[i][:, j, :])[:, halves, :, :])
 
-        def round_y_gpsimd(i, j, words):
+        def round_y_gpsimd(i, j, halves):
             nc.gpsimd.tensor_scalar(
-                out=rounded(i, j)[:, :, words, :],
-                in0=by_word_half(y_sb[i][:, j, :])[:, :, words, :],
+                out=rounded(i, j, halves),
+                in0=by_word_half(y_sb[i][:, j, :])[:, halves, :, :],
                 scalar1=1.0,
                 scalar2=-0.0,
                 op0=ALU.mult,
@@ -268,10 +268,10 @@ def tile_seatwise_crosstalk_canceller_k7_kernel(
             )
 
         def turn_y(i, j, bank):
-            words = y_rounded(i, j).bitcast(F32)
             for u in range(2):
                 col = (2 * j + u) * P
-                nc.tensor.transpose(bank[:, col : col + P], words[:, u * P : (u + 1) * P], ident[:])
+                words = y_rounded(i, j, slice(u, u + 1)).bitcast(F32)
+                nc.tensor.transpose(bank[:, col : col + P], words, ident[:])
 
         def frames(i, tiles):
             return slice(i * GROUP + tiles.start * P, i * GROUP + tiles.stop * P)
@@ -299,11 +299,8 @@ def tile_seatwise_crosstalk_canceller_k7_kernel(
 
         nc.gpsimd.memset(cs_raw[:].bitcast(I32), 0)
         make_identity(nc, ident[:])
-        nc.vector.memset(warm[:], 0.0)
-        nc.vector.memset(ceil_f32[:], 0.0)
         nc.vector.memset(hs_sb[:].rearrange("p g n -> p (g n)").bitcast(I32), 0)
-        for z in range(1, Z):
-            nc.vector.memset(cs_sb[z][:].bitcast(I32), 0)
+        nc.vector.memset(warm[:], 0.0)
 
         load_c(slice(0, 1))
         load_x(0)
@@ -334,53 +331,48 @@ def tile_seatwise_crosstalk_canceller_k7_kernel(
         load_x(5)
         load_bypass(1)
 
-        nc.scalar.copy(out=ceil_f32[0 : Z * PASSES, :], in_=ceil_rows[0 : Z * PASSES, :])
         turn_x(0, x_ps)
         turn_x(1, y_ps)
         gather_words(xg[0][:], x_ps, BOTH)
         gather_words(xg[1][:], y_ps, BOTH)
-        permute_c(0, 0)
-        permute_c(0, 1)
-        permute_c_scales(0)
-        permute_c_scales(1)
+        nc.scalar.copy(out=ceil_f32[0 : Z * PASSES, :], in_=ceil_rows[0 : Z * PASSES, :])
+        permute_c(0)
+        permute_c_scales()
         quantize_x(0)
         drive(0, 0)
         drive(0, 1)
         drive(0, 2)
-        permute_c(1, 0)
+        permute_c(1)
         quantize_x(1)
-        permute_c(1, 1)
-        permute_c(2, 0)
-        permute_c(2, 1)
-        permute_c(3, 0)
+        permute_c(2)
+        permute_c(3)
         limit(0, 0)
         drive(0, 3)
-        for t in range(4):
-            nc.tensor.transpose(ceil_ps[:, t * P : (t + 1) * P], ceil_f32[:, t : 512 : 4], ident[:])
         limit(0, 1)
-        limit(0, 2)
         drive(1, 0)
+        for t in range(4):
+            nc.tensor.transpose(ceil_ps[:, t : 512 : 4], ceil_f32[:, t : 512 : 4], ident[:])
+        limit(0, 2)
         drive(1, 1)
-        turn_x(2, x_ps)
-        turn_x(3, y_ps)
         limit(0, 3)
         drive(1, 2)
+        turn_x(2, x_ps)
+        turn_x(3, y_ps)
         for z in range(1, Z):
             shift_c_scales(z)
         apply_ceiling(0)
         limit(1, 0)
         drive(1, 3)
+        limit(1, 1)
         gather_words(xg[0][:], x_ps, BOTH)
         turn_x(4, x_ps)
-        limit(1, 1)
         limit(1, 2)
-        quantize_x(2)
         limit(1, 3)
+        quantize_x(2)
         drive(2, 0)
         drive(2, 1)
         gather_words(xg[1][:], y_ps, BOTH)
         quantize_d(0, BOTH)
-        permute_c(3, 1)
         load_x(6)
         load_bypass(2)
         load_h(1)
@@ -394,7 +386,7 @@ def tile_seatwise_crosstalk_canceller_k7_kernel(
             if k == 1:
                 quantize_x(3)
             if live(k - 3):
-                round_y_gpsimd(k - 3, 1, ALL_WORDS)
+                round_y_gpsimd(k - 3, 1, HIGH)
             if live(k - 2):
                 apply_gain(nc.gpsimd, k - 2, BOTH)
                 store_y(k - 2, BOTH)
@@ -433,9 +425,8 @@ def tile_seatwise_crosstalk_canceller_k7_kernel(
             if k + 1 == LAST:
                 store_scales(nc.sync, slice(0, (k - 2) * GROUP))
             if live(k - 2):
-                round_y(k - 2, 0, ALL_WORDS)
-            if k + 1 == LAST:
-                round_y(k - 2, 1, ALL_WORDS)
+                round_y(k - 2, 0, BOTH)
+                round_y(k - 2, 1, BOTH if k + 1 == LAST else LOW)
             if live(k + 6):
                 load_x(k + 6)
             if live(k + 2):
@@ -461,24 +452,24 @@ def tile_seatwise_crosstalk_canceller_k7_kernel(
         quantize_d(d, TILE1)
         room(d, 0)
         room(d, 1)
-        round_y(b, 0, ALL_WORDS)
-        round_y(b, 1, ALL_WORDS)
+        round_y(b, 0, BOTH)
+        round_y(b, 1, BOTH)
         turn_y(b, 0, y_ps)
         turn_y(b, 1, y_ps)
         apply_gain(nc.gpsimd, c, TILE0)
         add_bypass(c, 1)
         add_bypass(d, 0)
         add_bypass(d, 1)
-        round_y(c, 0, ALL_WORDS)
+        round_y(c, 0, BOTH)
         gather_words(yg[b % 4][:], y_ps, BOTH)
         apply_gain(nc.vector, c, TILE1)
         store_y(c, BOTH)
-        round_y(c, 1, ALL_WORDS)
+        round_y(c, 1, BOTH)
         turn_y(c, 0, y_ps)
         turn_y(c, 1, y_ps)
         apply_gain(nc.vector, d, TILE0)
         store_y(d, TILE0)
-        round_y(d, 0, ALL_WORDS)
+        round_y(d, 0, BOTH)
         apply_gain_rounded(d, 1)
         turn_y(d, 1, x_ps)
         turn_y(d, 0, x_ps)
@@ -490,6 +481,7 @@ def tile_seatwise_crosstalk_canceller_k7_kernel(
         quantize_y(b, BOTH)
         store_codes(slice(a * GROUP, c * GROUP))
         quantize_y(c, BOTH)
+        store_codes(frames(c, BOTH))
         quantize_y(d, BOTH)
-        store_codes(slice(c * GROUP, (d + 1) * GROUP))
+        store_codes(frames(d, BOTH))
         store_scales(nc.scalar, slice(a * GROUP, (d + 1) * GROUP))

@@ -62,7 +62,7 @@ def tile_seatwise_crosstalk_canceller_k7_kernel(
         cs_sb = [cs_first[:], c_raw[:, 0, 0:F], c_raw[:, 0, F : 2 * F], cs_raw[:]]
         h_sb = ring("h", Z, [P, PASSES, 2 * E], U8)
         hs_sb = sb.tile([P, Z * PASSES, E], U8, name="hs", align_bytes=64)
-        gain_sb = ring("gain", Z, [P, E], BF16)
+        gain_sb = sb.tile([P, Z * E], BF16, name="gain", align_bytes=64)
         ceil_rows = sb.tile([P, 512], BF16, name="ceil_rows", align_bytes=64)
         ceil_f32 = x_sb[0][:].rearrange("p j e -> p (j e)").bitcast(F32)
         xg = ring("xg", 2, [P, GROUP * 4], BF16)
@@ -100,8 +100,8 @@ def tile_seatwise_crosstalk_canceller_k7_kernel(
         def group_rows(rows, i):
             return rows[i * GROUP : (i + 1) * GROUP, :].rearrange("(j p) e -> p j e", p=P)
 
-        def load_x(i):
-            nc.sync.dma_start(out=x_sb[i][:], in_=group_rows(x_rows, i))
+        def load_x(engine, i):
+            engine.dma_start(out=x_sb[i][:], in_=group_rows(x_rows, i))
 
         def load_bypass(i):
             nc.sync.dma_start(out=bypass_sb[i][:], in_=group_rows(bypass_rows, i))
@@ -117,8 +117,11 @@ def tile_seatwise_crosstalk_canceller_k7_kernel(
                 in_=h_words[PASSES * z : PASSES * (z + 1)].rearrange("g p n -> p g n").bitcast(I32),
             )
 
-        def load_gain(z):
-            nc.sync.dma_start(out=gain_sb[z][:], in_=ear_gain[z].partition_broadcast(P))
+        def load_gain(seats):
+            cols = slice(seats.start * E, seats.stop * E)
+            nc.sync.dma_start(
+                out=gain_sb[:, cols], in_=ear_gain.rearrange("z e -> (z e)")[cols].partition_broadcast(P)
+            )
 
         def shift_c_scales(z):
             nc.sync.dma_start(
@@ -226,6 +229,18 @@ def tile_seatwise_crosstalk_canceller_k7_kernel(
                     stop=(g == PASSES - 1),
                 )
 
+        def keep_clock(bank, i, passes):
+            for n in range(passes):
+                nc.tensor.matmul_mx(
+                    out=bank[:],
+                    lhsT=d_codes[i % 2][:, 0, 0:P].bitcast(FP8X4),
+                    lhsT_scale=d_scales[i % 2][:, 0, 0:P],
+                    rhs=h_sb[Z - 1][:, 0, :].bitcast(FP4X4),
+                    rhs_scale=hs_sb[:, PASSES * (Z - 1), :],
+                    start=True,
+                    stop=True,
+                )
+
         def add_bypass(i, j):
             nc.vector.tensor_tensor(
                 out=s_sb[i % 2][:, j, :], in0=ear_bank(i, j)[:], in1=bypass_sb[i][:, j, :], op=ALU.add
@@ -236,7 +251,7 @@ def tile_seatwise_crosstalk_canceller_k7_kernel(
             engine.tensor_tensor(
                 out=y_sb[i][:, tiles, :],
                 in0=s_sb[i % 2][:, tiles, :],
-                in1=gain_sb[seat(i)][:].rearrange("p (j e) -> p j e", j=1).to_broadcast([P, count, E]),
+                in1=gain_sb[:, seat(i) * E : (seat(i) + 1) * E].rearrange("p (j e) -> p j e", j=1).to_broadcast([P, count, E]),
                 op=ALU.mult,
             )
 
@@ -250,7 +265,7 @@ def tile_seatwise_crosstalk_canceller_k7_kernel(
             nc.vector.tensor_tensor(
                 out=rounded(i, j, BOTH),
                 in0=by_word_half(s_sb[i % 2][:, j, :]),
-                in1=by_word_half(gain_sb[seat(i)][:]),
+                in1=by_word_half(gain_sb[:, seat(i) * E : (seat(i) + 1) * E]),
                 op=ALU.mult,
             )
 
@@ -299,37 +314,35 @@ def tile_seatwise_crosstalk_canceller_k7_kernel(
 
         nc.gpsimd.memset(cs_raw[:].bitcast(I32), 0)
         make_identity(nc, ident[:])
-        nc.vector.memset(hs_sb[:].rearrange("p g n -> p (g n)").bitcast(I32), 0)
         nc.vector.memset(warm[:], 0.0)
+        nc.vector.memset(hs_sb[:].rearrange("p g n -> p (g n)").bitcast(I32), 0)
 
         load_c(slice(0, 1))
-        load_x(0)
-        nc.scalar.dma_start(
-            out=ceil_rows[0 : Z * PASSES, :], in_=ceiling.rearrange("z (g f) -> (z g) f", g=PASSES)
-        )
+        load_x(nc.scalar, 0)
         for q in range(4):
-            nc.scalar.dma_start(
+            nc.sync.dma_start(
                 out=cs_raw[32 * q : 32 * q + 16, :].bitcast(I32),
                 in_=c_scales[:, 4 * q : 4 * q + 4, :].bitcast(I32),
             )
+        nc.scalar.dma_start(
+            out=ceil_rows[0 : Z * PASSES, :], in_=ceiling.rearrange("z (g f) -> (z g) f", g=PASSES)
+        )
         nc.scalar.activation(out=warm[:], in_=warm[:], func=ACT.Tanh)
-        load_x(1)
+        load_x(nc.sync, 1)
         load_c(slice(1, 2))
         load_c(slice(2, 3))
-        load_x(2)
+        load_x(nc.sync, 2)
         load_c(slice(3, 4))
-        load_x(3)
+        load_x(nc.sync, 3)
         for q in range(4):
             nc.sync.dma_start(
                 out=hs_sb[32 * q : 32 * q + 4, :, :].bitcast(I32),
                 in_=h_scales[:, 4 * q : 4 * q + 4, :].rearrange("g r n -> r g n").bitcast(I32),
             )
         load_h(0)
-        load_x(4)
+        load_x(nc.sync, 4)
         load_bypass(0)
-        load_gain(0)
-        load_x(5)
-        load_bypass(1)
+        load_x(nc.sync, 5)
 
         turn_x(0, x_ps)
         turn_x(1, y_ps)
@@ -360,6 +373,8 @@ def tile_seatwise_crosstalk_canceller_k7_kernel(
         turn_x(3, y_ps)
         for z in range(1, Z):
             shift_c_scales(z)
+        load_gain(slice(0, 1))
+        load_bypass(1)
         apply_ceiling(0)
         limit(1, 0)
         drive(1, 3)
@@ -373,10 +388,9 @@ def tile_seatwise_crosstalk_canceller_k7_kernel(
         drive(2, 1)
         gather_words(xg[1][:], y_ps, BOTH)
         quantize_d(0, BOTH)
-        load_x(6)
+        load_x(nc.sync, 6)
         load_bypass(2)
         load_h(1)
-        load_gain(1)
 
         def live(i):
             return 0 <= i < GROUPS
@@ -428,14 +442,16 @@ def tile_seatwise_crosstalk_canceller_k7_kernel(
                 round_y(k - 2, 0, BOTH)
                 round_y(k - 2, 1, BOTH if k + 1 == LAST else LOW)
             if live(k + 6):
-                load_x(k + 6)
+                load_x(nc.sync, k + 6)
             if live(k + 2):
                 load_bypass(k + 2)
             if k in (3, 6):
                 load_h(k // 3 + 1)
-                load_gain(k // 3 + 1)
+            if k == 2:
+                load_gain(slice(1, Z))
 
         a, b, c, d = LAST - 3, LAST - 2, LAST - 1, LAST
+        keep_clock(v_ps[0], b, 2)
         room(c, 0)
         turn_y(a, 0, y_ps)
         turn_y(a, 1, y_ps)
@@ -444,6 +460,7 @@ def tile_seatwise_crosstalk_canceller_k7_kernel(
         apply_gain(nc.gpsimd, b, BOTH)
         store_y(b, BOTH)
         gather_words(yg[a % 4][:], y_ps, BOTH)
+        keep_clock(y_ps, c, 3)
         apply_ceiling_part(d, 1, 0)
         apply_ceiling_part(d, 0, 1)
         apply_ceiling_part(d, 1, 1)

from contextlib import ExitStack

import concourse.mybir as mybir
from concourse.masks import make_identity

Z, R, E, F = 4, 768, 512, 1024
FLOPS = 2 * 2 * Z * R * E * F

F32 = mybir.dt.float32
BF16 = mybir.dt.bfloat16
I32 = mybir.dt.int32
U32 = mybir.dt.uint32
U8 = mybir.dt.uint8
FP8X4 = mybir.dt.float8_e4m3fn_x4
FP4X4 = mybir.dt.float4_e2m1fn_x4
ACT = mybir.ActivationFunctionType
ALU = mybir.AluOpType

P = 128
GROUP = 256
TILES = GROUP // P
GROUPS = Z * R // GROUP
GROUPS_PER_SEAT = R // GROUP
PASSES = F // 512
DRIVE_BANKS = 3
SHIFT_ROWS = 112
LAST = GROUPS - 1
BOTH = slice(0, TILES)
TILE0 = slice(0, 1)
TILE1 = slice(1, 2)
LOW = slice(0, 1)
HIGH = slice(1, 2)


def tile_seatwise_crosstalk_canceller_k7_kernel(
    tc, x, c_words, c_scales, ceiling, h_words, h_scales, bypass, ear_gain, out_0, out_1, out_2
):
    nc = tc.nc
    x_rows = x.rearrange("z r e -> (z r) e")
    bypass_rows = bypass.rearrange("z r e -> (z r) e")
    y_rows = out_0.rearrange("z r e -> (z r) e")
    y_words = out_1[0].rearrange("p m t -> p (m t)").bitcast(I32)
    y_scale_rows = out_2[0]

    with ExitStack() as ctx:
        sb = ctx.enter_context(tc.tile_pool(name="sb", bufs=1))
        ps = ctx.enter_context(tc.psum_pool(name="ps", bufs=1))
        ctx.enter_context(tc.manual_schedule())

        def ring(name, count, shape, dtype):
            return [sb.tile(shape, dtype, name="%s%d" % (name, i), align_bytes=64) for i in range(count)]

        ident = sb.tile([P, P], F32, name="ident", align_bytes=64)
        warm = sb.tile([P, 1], F32, name="warm", align_bytes=64)
        x_sb = ring("x", GROUPS, [P, TILES, E], BF16)
        bypass_sb = ring("bypass", GROUPS, [P, TILES, E], BF16)
        y_sb = ring("y", GROUPS, [P, TILES, E], F32)
        c_raw = sb.tile([P, Z, 2 * F], U8, name="c_raw", align_bytes=64)
        c_sb = ring("c", Z, [P, 2 * F], U8)
        cs_raw = sb.tile([P, F], U8, name="cs_raw", align_bytes=64)
        cs_first = sb.tile([P, F], U8, name="cs_first", align_bytes=64)
        cs_sb = [cs_first[:], c_raw[:, 0, 0:F], c_raw[:, 0, F : 2 * F], cs_raw[:]]
        h_sb = ring("h", Z, [P, PASSES, 2 * E], U8)
        hs_sb = sb.tile([P, Z * PASSES, E], U8, name="hs", align_bytes=64)
        gain_sb = sb.tile([P, Z * E], BF16, name="gain", align_bytes=64)
        ceil_rows = sb.tile([P, 512], BF16, name="ceil_rows", align_bytes=64)
        ceil_f32 = x_sb[0][:].rearrange("p j e -> p (j e)").bitcast(F32)
        xg = ring("xg", 2, [P, GROUP * 4], BF16)
        x_codes = ring("x_codes", 4, [P, GROUP], U32)
        x_scales = ring("x_scales", 4, [P, GROUP], U8)
        th = ring("th", 2, [P, 2, PASSES, GROUP, 2], F32)
        d_bf = ring("d_bf", 2, [P, PASSES, GROUP * 4], BF16)
        d_codes = ring("d_codes", 2, [P, PASSES, GROUP], U32)
        d_scales = ring("d_scales", 2, [P, PASSES, GROUP], U8)
        s_sb = ring("s", 2, [P, TILES, E], F32)
        y_bf = ring("y_bf", 2, [P, TILES, E], BF16)
        yg = ring("yg", 4, [P, GROUP * 4], BF16)
        y_codes = sb.tile([P, Z * R], U32, name="y_codes", align_bytes=64)
        y_scales = sb.tile([P, Z * R], U8, name="y_scales", align_bytes=64)

        ceil_ps = ps.tile([P, 512], F32, name="ceil_ps")
        x_ps = ps.tile([P, 512], F32, name="x_ps")
        y_ps = ps.tile([P, 512], F32, name="y_ps")
        u_ps = [ps.tile([P, 512], F32, name="u_ps%d" % i) for i in range(DRIVE_BANKS)]
        v_ps = [ps.tile([P, 512], F32, name="v_ps%d" % i) for i in range(TILES)]

        def d_stage(i):
            if i in (1, LAST - 1, LAST):
                return y_sb[i - 1][:].bitcast(BF16)
            return d_bf[i % 2][:]

        def y_rounded(i, j, halves):
            if j == 1 and halves == HIGH and i < LAST - 3:
                return d_stage(i + 2)[:, 0, 0 : E // 2]
            return y_bf[i % 2][:, j, halves.start * (E // 2) : halves.stop * (E // 2)]

        def seat(i):
            return i // GROUPS_PER_SEAT

        def group_rows(rows, i):
            return rows[i * GROUP : (i + 1) * GROUP, :].rearrange("(j p) e -> p j e", p=P)

        def load_x(engine, i):
            engine.dma_start(out=x_sb[i][:], in_=group_rows(x_rows, i))

        def load_bypass(i):
            nc.sync.dma_start(out=bypass_sb[i][:], in_=group_rows(bypass_rows, i))

        def load_c(seats):
            nc.sync.dma_start(
                out=c_raw[:, seats, :].bitcast(I32), in_=c_words[seats].rearrange("z p n -> p z n").bitcast(I32)
            )

        def load_h(z):
            nc.sync.dma_start(
                out=h_sb[z][:].bitcast(I32),
                in_=h_words[PASSES * z : PASSES * (z + 1)].rearrange("g p n -> p g n").bitcast(I32),
            )

        def load_gain(seats):
            cols = slice(seats.start * E, seats.stop * E)
            nc.sync.dma_start(
                out=gain_sb[:, cols], in_=ear_gain.rearrange("z e -> (z e)")[cols].partition_broadcast(P)
            )

        def shift_c_scales(z):
            nc.sync.dma_start(
                out=cs_sb[z][0:SHIFT_ROWS, :].bitcast(I32),
                in_=cs_sb[0][4 * z : 4 * z + SHIFT_ROWS, :].bitcast(I32),
            )

        def permute_c(z):
            nc.vector.tensor_copy(
                out=c_sb[z][:].rearrange("p (g t m b) -> p g t m b", g=PASSES, t=4, b=2),
                in_=c_raw[:, z, :].rearrange("p (g m t b) -> p g t m b", g=PASSES, t=4, b=2),
            )

        def permute_c_scales():
            nc.vector.tensor_copy(
                out=cs_sb[0].rearrange("p (g t m) -> p g t m", g=PASSES, t=4),
                in_=cs_raw[:].rearrange("p (g m t) -> p g t m", g=PASSES, t=4),
            )

        def turn_x(i, bank):
            for j in range(TILES):
                words = x_sb[i][:, j, :].bitcast(F32)
                for u in range(2):
                    col = (2 * j + u) * P
                    nc.tensor.transpose(bank[:, col : col + P], words[:, u : 2 * P : 2], ident[:])

        def gather_words(dst, bank, tiles):
            nc.scalar.copy(
                out=dst.bitcast(F32).rearrange("p (j r u) -> p j r u", j=TILES, u=2)[:, tiles],
                in_=bank[:].rearrange("p (j u r) -> p j r u", j=TILES, u=2)[:, tiles],
            )

        def quantize_x(i):
            nc.vector.quantize_mx(out=x_codes[i % 4][:].bitcast(FP8X4), scales=x_scales[i % 4][:], in_=xg[i % 2][:])

        def drive(i, b):
            z, g, u = seat(i), b // 2, b % 2
            bank = u_ps[(4 * i + b) % DRIVE_BANKS]
            for e in range(2):
                col = g * 512 + (2 * u + e) * P
                nc.tensor.matmul_mx(
                    out=bank[:, e * GROUP : (e + 1) * GROUP],
                    lhsT=c_sb[z][:, 2 * col : 2 * (col + P)].bitcast(FP4X4),
                    lhsT_scale=cs_sb[z][:, col : col + P],
                    rhs=x_codes[i % 4][:].bitcast(FP8X4),
                    rhs_scale=x_scales[i % 4][:],
                    start=True,
                    stop=True,
                )

        def limit(i, b):
            bank = u_ps[(4 * i + b) % DRIVE_BANKS]
            nc.scalar.activation(
                out=th[i % 2][:, b % 2, b // 2, :, :],
                in_=bank[:].rearrange("p (e n) -> p n e", e=2),
                func=ACT.Tanh,
            )

        def d_part(ap, i, g, j):
            width = ap.shape[2] // TILES
            if i == LAST:
                return ap[:, j, g * width : (g + 1) * width]
            return ap[:, g, j * width : (j + 1) * width]

        def apply_ceiling(i):
            rows = slice(PASSES * seat(i), PASSES * (seat(i) + 1))
            ceil = ceil_ps[:].rearrange("p (r n t) -> p r n t", t=4, n=1)[:, rows, :, :]
            nc.vector.tensor_tensor(
                out=d_stage(i).rearrange("p g (n t) -> p g n t", t=4),
                in0=th[i % 2][:].rearrange("p u g n e -> p (g n) u e"),
                in1=ceil.to_broadcast([P, PASSES, GROUP, 4]),
                op=ALU.mult,
            )

        def apply_ceiling_part(i, g, j):
            row = PASSES * seat(i) + g
            ceil = ceil_ps[:].rearrange("p (r u e) -> p r u e", u=2, e=2)[:, row : row + 1, :, :]
            nc.vector.tensor_tensor(
                out=d_part(d_stage(i), i, g, j).rearrange("p (n u e) -> p n u e", u=2, e=2),
                in0=th[i % 2][:, :, g, j * P : (j + 1) * P, :].rearrange("p u n e -> p n u e"),
                in1=ceil.to_broadcast([P, P, 2, 2]),
                op=ALU.mult,
            )

        def quantize_d(i, halves):
            nc.vector.quantize_mx(
                out=d_codes[i % 2][:, halves, :].rearrange("p a n -> p (a n)").bitcast(FP8X4),
                scales=d_scales[i % 2][:, halves, :].rearrange("p a n -> p (a n)"),
                in_=d_stage(i)[:, halves, :].rearrange("p a n -> p (a n)"),
            )

        def ear_bank(i, j):
            return u_ps[1] if (i, j) == (LAST, 1) else v_ps[j]

        def room(i, j):
            z = seat(i)
            for g in range(PASSES):
                nc.tensor.matmul_mx(
                    out=ear_bank(i, j)[:],
                    lhsT=d_part(d_codes[i % 2][:], i, g, j).bitcast(FP8X4),
                    lhsT_scale=d_part(d_scales[i % 2][:], i, g, j),
                    rhs=h_sb[z][:, g, :].bitcast(FP4X4),
                    rhs_scale=hs_sb[:, PASSES * z + g, :],
                    start=(g == 0),
                    stop=(g == PASSES - 1),
                )

        def keep_clock(bank, i, passes):
            for n in range(passes):
                nc.tensor.matmul_mx(
                    out=bank[:],
                    lhsT=d_codes[i % 2][:, 0, 0:P].bitcast(FP8X4),
                    lhsT_scale=d_scales[i % 2][:, 0, 0:P],
                    rhs=h_sb[Z - 1][:, 0, :].bitcast(FP4X4),
                    rhs_scale=hs_sb[:, PASSES * (Z - 1), :],
                    start=True,
                    stop=True,
                )

        def add_bypass(i, j):
            nc.vector.tensor_tensor(
                out=s_sb[i % 2][:, j, :], in0=ear_bank(i, j)[:], in1=bypass_sb[i][:, j, :], op=ALU.add
            )

        def apply_gain(engine, i, tiles):
            count = tiles.stop - tiles.start
            engine.tensor_tensor(
                out=y_sb[i][:, tiles, :],
                in0=s_sb[i % 2][:, tiles, :],
                in1=gain_sb[:, seat(i) * E : (seat(i) + 1) * E].rearrange("p (j e) -> p j e", j=1).to_broadcast([P, count, E]),
                op=ALU.mult,
            )

        def by_word_half(ap):
            return ap.rearrange("p (m u e) -> p u m e", u=2, e=2)

        def rounded(i, j, halves):
            return y_rounded(i, j, halves).rearrange("p (u m e) -> p u m e", m=P, e=2)

        def apply_gain_rounded(i, j):
            nc.vector.tensor_tensor(
                out=rounded(i, j, BOTH),
                in0=by_word_half(s_sb[i % 2][:, j, :]),
                in1=by_word_half(gain_sb[:, seat(i) * E : (seat(i) + 1) * E]),
                op=ALU.mult,
            )

        def round_y(i, j, halves):
            nc.scalar.copy(out=rounded(i, j, halves), in_=by_word_half(y_sb[i][:, j, :])[:, halves, :, :])

        def round_y_gpsimd(i, j, halves):
            nc.gpsimd.tensor_scalar(
                out=rounded(i, j, halves),
                in0=by_word_half(y_sb[i][:, j, :])[:, halves, :, :],
                scalar1=1.0,
                scalar2=-0.0,
                op0=ALU.mult,
                op1=ALU.add,
            )

        def turn_y(i, j, bank):
            for u in range(2):
                col = (2 * j + u) * P
                words = y_rounded(i, j, slice(u, u + 1)).bitcast(F32)
                nc.tensor.transpose(bank[:, col : col + P], words, ident[:])

        def frames(i, tiles):
            return slice(i * GROUP + tiles.start * P, i * GROUP + tiles.stop * P)

        def quantize_y(i, tiles):
            cols = frames(i, tiles)
            nc.vector.quantize_mx(
                out=y_codes[:, cols].bitcast(FP8X4),
                scales=y_scales[:, cols],
                in_=yg[i % 4][:, tiles.start * 4 * P : tiles.stop * 4 * P],
            )

        def store_y(i, tiles):
            nc.sync.dma_start(out=group_rows(y_rows, i)[:, tiles, :], in_=y_sb[i][:, tiles, :])

        def store_codes(cols):
            nc.sync.dma_start(out=y_words[:, cols], in_=y_codes[:, cols].bitcast(I32))

        def store_scales(engine, cols):
            for q in range(4):
                engine.dma_start(
                    out=y_scale_rows[4 * q : 4 * q + 4, cols].bitcast(I32),
                    in_=y_scales[32 * q : 32 * q + 4, cols].bitcast(I32),
                )

        nc.gpsimd.memset(cs_raw[:].bitcast(I32), 0)
        make_identity(nc, ident[:])
        nc.vector.memset(warm[:], 0.0)
        nc.vector.memset(hs_sb[:].rearrange("p g n -> p (g n)").bitcast(I32), 0)

        load_c(slice(0, 1))
        load_x(nc.scalar, 0)
        for q in range(4):
            nc.sync.dma_start(
                out=cs_raw[32 * q : 32 * q + 16, :].bitcast(I32),
                in_=c_scales[:, 4 * q : 4 * q + 4, :].bitcast(I32),
            )
        nc.scalar.dma_start(
            out=ceil_rows[0 : Z * PASSES, :], in_=ceiling.rearrange("z (g f) -> (z g) f", g=PASSES)
        )
        nc.scalar.activation(out=warm[:], in_=warm[:], func=ACT.Tanh)
        load_x(nc.sync, 1)
        load_c(slice(1, 2))
        load_c(slice(2, 3))
        load_x(nc.sync, 2)
        load_c(slice(3, 4))
        load_x(nc.sync, 3)
        for q in range(4):
            nc.sync.dma_start(
                out=hs_sb[32 * q : 32 * q + 4, :, :].bitcast(I32),
                in_=h_scales[:, 4 * q : 4 * q + 4, :].rearrange("g r n -> r g n").bitcast(I32),
            )
        load_h(0)
        load_x(nc.sync, 4)
        load_bypass(0)
        load_x(nc.sync, 5)

        turn_x(0, x_ps)
        turn_x(1, y_ps)
        gather_words(xg[0][:], x_ps, BOTH)
        gather_words(xg[1][:], y_ps, BOTH)
        nc.scalar.copy(out=ceil_f32[0 : Z * PASSES, :], in_=ceil_rows[0 : Z * PASSES, :])
        permute_c(0)
        permute_c_scales()
        quantize_x(0)
        drive(0, 0)
        drive(0, 1)
        drive(0, 2)
        permute_c(1)
        quantize_x(1)
        permute_c(2)
        permute_c(3)
        limit(0, 0)
        drive(0, 3)
        limit(0, 1)
        drive(1, 0)
        for t in range(4):
            nc.tensor.transpose(ceil_ps[:, t : 512 : 4], ceil_f32[:, t : 512 : 4], ident[:])
        limit(0, 2)
        drive(1, 1)
        limit(0, 3)
        drive(1, 2)
        turn_x(2, x_ps)
        turn_x(3, y_ps)
        for z in range(1, Z):
            shift_c_scales(z)
        load_gain(slice(0, 1))
        load_bypass(1)
        apply_ceiling(0)
        limit(1, 0)
        drive(1, 3)
        limit(1, 1)
        gather_words(xg[0][:], x_ps, BOTH)
        turn_x(4, x_ps)
        limit(1, 2)
        limit(1, 3)
        quantize_x(2)
        drive(2, 0)
        drive(2, 1)
        gather_words(xg[1][:], y_ps, BOTH)
        quantize_d(0, BOTH)
        load_x(nc.sync, 6)
        load_bypass(2)
        load_h(1)

        def live(i):
            return 0 <= i < GROUPS

        for k in range(1, LAST):
            apply_ceiling(k)
            if k == 1:
                quantize_x(3)
            if live(k - 3):
                round_y_gpsimd(k - 3, 1, HIGH)
            if live(k - 2):
                apply_gain(nc.gpsimd, k - 2, BOTH)
                store_y(k - 2, BOTH)
            if live(k + 3):
                gather_words(xg[(k + 3) % 2][:], x_ps, BOTH)
            limit(k + 1, 0)
            limit(k + 1, 1)
            if live(k - 1):
                room(k - 1, 0)
            drive(k + 1, 2)
            if live(k - 3):
                turn_y(k - 3, 0, y_ps)
                turn_y(k - 3, 1, y_ps)
                gather_words(yg[(k - 3) % 4][:], y_ps, BOTH)
            if live(k - 1):
                room(k - 1, 1)
            drive(k + 1, 3)
            if live(k + 4):
                turn_x(k + 4, x_ps)
            limit(k + 1, 2)
            limit(k + 1, 3)
            if live(k - 1):
                add_bypass(k - 1, 0)
                add_bypass(k - 1, 1)
            if live(k + 2):
                drive(k + 2, 0)
                drive(k + 2, 1)
            if live(k + 3) and k >= 3:
                quantize_x(k + 3)
            quantize_d(k, BOTH)
            if k < 3:
                quantize_x(k + 3)
            if live(k - 3):
                quantize_y(k - 3, BOTH)
                store_codes(frames(k - 3, BOTH))
            if k + 1 == LAST:
                store_scales(nc.sync, slice(0, (k - 2) * GROUP))
            if live(k - 2):
                round_y(k - 2, 0, BOTH)
                round_y(k - 2, 1, BOTH if k + 1 == LAST else LOW)
            if live(k + 6):
                load_x(nc.sync, k + 6)
            if live(k + 2):
                load_bypass(k + 2)
            if k in (3, 6):
                load_h(k // 3 + 1)
            if k == 2:
                load_gain(slice(1, Z))

        a, b, c, d = LAST - 3, LAST - 2, LAST - 1, LAST
        keep_clock(v_ps[0], b, 2)
        room(c, 0)
        turn_y(a, 0, y_ps)
        turn_y(a, 1, y_ps)
        room(c, 1)
        apply_ceiling_part(d, 0, 0)
        apply_gain(nc.gpsimd, b, BOTH)
        store_y(b, BOTH)
        gather_words(yg[a % 4][:], y_ps, BOTH)
        keep_clock(y_ps, c, 3)
        apply_ceiling_part(d, 1, 0)
        apply_ceiling_part(d, 0, 1)
        apply_ceiling_part(d, 1, 1)
        add_bypass(c, 0)
        quantize_d(d, TILE0)
        quantize_d(d, TILE1)
        room(d, 0)
        room(d, 1)
        round_y(b, 0, BOTH)
        round_y(b, 1, BOTH)
        turn_y(b, 0, y_ps)
        turn_y(b, 1, y_ps)
        apply_gain(nc.gpsimd, c, TILE0)
        add_bypass(c, 1)
        add_bypass(d, 0)
        add_bypass(d, 1)
        round_y(c, 0, BOTH)
        gather_words(yg[b % 4][:], y_ps, BOTH)
        apply_gain(nc.vector, c, TILE1)
        store_y(c, BOTH)
        round_y(c, 1, BOTH)
        turn_y(c, 0, y_ps)
        turn_y(c, 1, y_ps)
        apply_gain(nc.vector, d, TILE0)
        store_y(d, TILE0)
        round_y(d, 0, BOTH)
        apply_gain_rounded(d, 1)
        turn_y(d, 1, x_ps)
        turn_y(d, 0, x_ps)
        gather_words(yg[c % 4][:], y_ps, BOTH)
        apply_gain(nc.vector, d, TILE1)
        store_y(d, TILE1)
        gather_words(yg[d % 4][:], x_ps, BOTH)
        quantize_y(a, BOTH)
        quantize_y(b, BOTH)
        store_codes(slice(a * GROUP, c * GROUP))
        quantize_y(c, BOTH)
        store_codes(frames(c, BOTH))
        quantize_y(d, BOTH)
        store_codes(frames(d, BOTH))
        store_scales(nc.scalar, slice(a * GROUP, (d + 1) * GROUP))
